import numpy as np
import ml_dtypes


def mxq(x, axis, fmt="e4m3"):
    dtype, down = {"e4m3": (ml_dtypes.float8_e4m3fn, 7), "e5m2": (ml_dtypes.float8_e5m2, 14)}[fmt]
    v = np.moveaxis(np.asarray(x, np.float32).astype(ml_dtypes.bfloat16).astype(np.float64), axis, -1)
    blocks = v.reshape(v.shape[:-1] + (-1, 32))
    amax = np.abs(blocks).max(-1, keepdims=True)
    byte = np.maximum(np.where(amax > 0, np.frexp(amax)[1] - 1 + 127, 0) - down, 1)
    scale = np.exp2(byte - 127.0)
    codes = (blocks / scale).astype(np.float32).astype(dtype).astype(np.float64)
    return np.moveaxis((codes * scale).reshape(v.shape), -1, axis)


WIDE = False


def mx_kscale(k):
    if not WIDE:
        return np.ones(k)
    levels = np.array([24, -24, 12, -12, 0])
    if k % 512:
        return np.exp2(np.random.permutation(np.resize(levels, k // 32))).repeat(32)
    a = np.empty((k // 512, 16))
    for p in range(k // 512):
        a[p, :8] = np.random.permutation(np.resize(levels, 8))
        for g in range(8):
            far = levels[np.abs(levels - a[p, g]) >= 10]
            a[p, g + 8] = far[np.random.randint(len(far))]
    return np.exp2(a.ravel()).repeat(32)


def f64(x):
    return np.asarray(x).astype(np.float64)


def striped(idx):
    return np.tile(idx.reshape(-1, 16).T, (8, 1)).astype(np.uint16)


def unstriped(offs):
    return offs[:16].T.reshape(-1).astype(np.int64)


E2M1 = np.array([0.0, 0.5, 1.0, 1.5, 2.0, 3.0, 4.0, 6.0, -0.0, -0.5, -1.0, -1.5, -2.0, -3.0, -4.0, -6.0])


def pack_weight(w, fmt):
    k, n = w.shape
    w = f64(np.asarray(w, np.float32).astype(ml_dtypes.bfloat16)).reshape(k // 32, 32, n)
    amax = np.abs(w).max(1)
    if fmt == "e4m3":
        byte = np.frexp(amax)[1] - 1 + 127 - 7
    else:
        mant, ex = np.frexp(amax / 6.0)
        byte = np.where(mant > 0.5, ex, ex - 1) + 127
    byte = np.clip(np.where(amax > 0, byte, 1), 1, 254)
    scaled = (w * np.exp2(127.0 - byte)[:, None, :]).reshape(k, n).astype(np.float32)
    by_word = np.ascontiguousarray(scaled.reshape(k // 512, 128, 4, n).transpose(0, 1, 3, 2))
    if fmt == "e4m3":
        words = by_word.astype(ml_dtypes.float8_e4m3fn).view(np.uint8)
    else:
        c = by_word.astype(ml_dtypes.float4_e2m1fn).view(np.uint8) & 0xF
        words = (c[..., 0::2] | (c[..., 1::2] << 4)).reshape(k // 512, 128, 2 * n)
    return np.ascontiguousarray(words), np.ascontiguousarray(byte.astype(np.uint8).reshape(k // 512, 16, n))


def unpack_weight(words, scales, fmt):
    g, _, n = scales.shape
    words = np.ascontiguousarray(words).reshape(g, 128, n, -1)
    if fmt == "e4m3":
        vals = words.view(ml_dtypes.float8_e4m3fn).astype(np.float64)
    else:
        nib = np.empty((g, 128, n, 4), np.uint8)
        nib[..., 0::2] = words & 0xF
        nib[..., 1::2] = words >> 4
        vals = E2M1[nib]
    vals = vals * np.repeat(np.exp2(scales.astype(np.float64) - 127.0), 8, axis=1)[..., None]
    return vals.transpose(0, 1, 3, 2).reshape(g * 512, n)


def planes(y):
    n, m = y.shape
    v = y.astype(np.float32).astype(ml_dtypes.bfloat16).astype(np.float64).reshape(n // 32, 32, m)
    top = np.abs(v).max(1)
    byte = np.clip(np.where(top > 0, np.frexp(top)[1] - 1 + 127 - 7, 1), 1, 254)
    codes = (v * np.exp2(127.0 - byte)[:, None, :]).reshape(n, m).astype(np.float32).astype(ml_dtypes.float8_e4m3fn).view(np.uint8)
    words = codes.reshape(n // 512, 128, 4, m).transpose(0, 1, 3, 2)
    return np.ascontiguousarray(words), np.ascontiguousarray(byte.astype(np.uint8).reshape(n // 512, 16, m))


def sigm(f):
    return 1.0 / (1.0 + np.exp(-np.maximum(f, -700.0)))


K, N, T, J = 512, 512, 4096, 1024


def setup_inputs():
    n = np.random.standard_normal
    s = mx_kscale(K)[:, None]
    p_tab = pack_weight(n((K, T)) * s, "e4m3")
    p_wg = pack_weight(n((K, N)) / np.sqrt(K) / s, "e4m3")
    p_wh4 = pack_weight(n((K, N)) / np.sqrt(K) / s, "e2m1")
    return {
        "tab_words": p_tab[0],
        "tab_scales": p_tab[1],
        "wg_words": p_wg[0],
        "wg_scales": p_wg[1],
        "wh4_words": p_wh4[0],
        "wh4_scales": p_wh4[1],
        "whd": (0.4 * (n((K, N)) / np.sqrt(K) / s)).astype(np.float32),
        "bg": (0.3 * n(N) - 1.0).astype(np.float32),
        "rT": (n((N, T))).astype(np.float32),
        "offs": striped(np.random.permutation(T)[:J]),
    }


def reference(tab_words, tab_scales, wg_words, wg_scales, wh4_words, wh4_scales, whd, bg, rT, offs):
    idx = unstriped(offs)
    tab_ = unpack_weight(tab_words, tab_scales, "e4m3")[:, idx]
    wg_ = unpack_weight(wg_words, wg_scales, "e4m3")
    wh4_ = unpack_weight(wh4_words, wh4_scales, "e2m1")
    whd_ = mxq(f64(whd), 0, "e4m3")
    ga = wg_.T @ tab_
    gate = sigm(ga + f64(bg)[:, None])
    ha = wh4_.T @ tab_ + whd_.T @ tab_
    out_0 = f64(rT)[:, idx] + gate * (np.maximum(ha, 0.0) - f64(rT)[:, idx])
    return (out_0,) + planes(out_0)

@@ -1,0 +1,204 @@
+from contextlib import ExitStack
+
+import concourse.mybir as mybir
+
+K, N, T, J = 512, 512, 4096, 1024
+FLOPS = 3 * 2 * K * N * J
+
+F32 = mybir.dt.float32
+BF16 = mybir.dt.bfloat16
+I32 = mybir.dt.int32
+U32 = mybir.dt.uint32
+U16 = mybir.dt.uint16
+U8 = mybir.dt.uint8
+FP8X4 = mybir.dt.float8_e4m3fn_x4
+FP4X4 = mybir.dt.float4_e2m1fn_x4
+ACT = mybir.ActivationFunctionType
+ALU = mybir.AluOpType
+
+P = 128
+PACK = 4
+HALF = 512
+TAIL = (256, 256, 256, 256)
+
+
+def load_scale_rows(queue, plane, rows):
+    for q in range(4):
+        queue.dma_start(out=plane[32 * q : 32 * q + 4, :].bitcast(I32), in_=rows[0, 4 * q : 4 * q + 4, :].bitcast(I32))
+
+
+def tile_list_hwayt_dl_reluP_kernel(
+    tc, tab_words, tab_scales, wg_words, wg_scales, wh4_words, wh4_scales, whd, bg, rT, offs, out_0, out_1, out_2
+):
+    nc = tc.nc
+    with ExitStack() as ctx:
+        keep = ctx.enter_context(tc.tile_pool(name="keep", bufs=1))
+        ring = ctx.enter_context(tc.tile_pool(name="ring", bufs=2))
+        psum_g = ctx.enter_context(tc.psum_pool(name="psum_g", bufs=3))
+        psum_h = ctx.enter_context(tc.psum_pool(name="psum_h", bufs=5))
+
+        offsets = keep.tile([P, J // 16], U16, name="offsets")
+        nc.sync.dma_start(offsets[:], offs)
+
+        tab_s = keep.tile([P, T], U8, name="tab_s", align_bytes=64)
+        nc.vector.memset(tab_s[:].bitcast(I32), 0)
+        wg_s_raw = keep.tile([P, N], U8, name="wg_s_raw", align_bytes=64)
+        wh4_s_raw = keep.tile([P, N], U8, name="wh4_s_raw", align_bytes=64)
+        nc.vector.memset(wg_s_raw[:].bitcast(I32), 0)
+        nc.vector.memset(wh4_s_raw[:].bitcast(I32), 0)
+
+        warm = keep.tile([P, 1], F32, name="warm")
+        warm2 = keep.tile([P, 1], F32, name="warm2")
+        nc.vector.memset(warm[:], 0.0)
+        nc.scalar.activation(warm2[:], warm[:], ACT.Sigmoid)
+
+        wg_raw = keep.tile([P, N], U32, name="wg_raw", align_bytes=64)
+        nc.sync.dma_start(out=wg_raw[:].bitcast(I32), in_=wg_words[0].rearrange("p n i -> p (n i)").bitcast(I32))
+        wh4_raw = keep.tile([P, 2 * N], U8, name="wh4_raw", align_bytes=64)
+        nc.sync.dma_start(out=wh4_raw[:].bitcast(I32), in_=wh4_words[0].bitcast(I32))
+        load_scale_rows(nc.sync, tab_s, tab_scales)
+        whd_raw = keep.tile([P, PACK, N], F32, name="whd_raw")
+        nc.sync.dma_start(out=whd_raw[:], in_=whd.rearrange("(p i) n -> p i n", i=PACK))
+        load_scale_rows(nc.sync, wg_s_raw, wg_scales)
+        tab_w = keep.tile([P, T], U32, name="tab_w", align_bytes=64)
+        nc.sync.dma_start(out=tab_w[:].bitcast(I32), in_=tab_words[0].rearrange("p n i -> p (n i)").bitcast(I32))
+        bias = keep.tile([P, PACK], F32, name="bias")
+        nc.sync.dma_start(out=bias[:], in_=bg.rearrange("(p t) -> p t", t=PACK))
+        load_scale_rows(nc.sync, wh4_s_raw, wh4_scales)
+        r_rows = rT.rearrange("(p t) c -> t p c", t=PACK)
+        r_tab = []
+        for t in range(PACK):
+            r_t = keep.tile([P, T], F32, name=f"r_tab{t}")
+            nc.sync.dma_start(out=r_t[:], in_=r_rows[t])
+            r_tab.append(r_t)
+
+        wg_w = keep.tile([P, N], U32, name="wg_w", align_bytes=64)
+        nc.vector.tensor_copy(
+            out=wg_w[:].bitcast(I32).rearrange("p (t m) -> p m t", t=PACK),
+            in_=wg_raw[:].bitcast(I32).rearrange("p (m t) -> p m t", t=PACK),
+        )
+        wh4_w = keep.tile([P, 2 * N], U8, name="wh4_w", align_bytes=64)
+        nc.vector.tensor_copy(
+            out=wh4_w[:].rearrange("p (t m b) -> p m t b", t=PACK, b=2),
+            in_=wh4_raw[:].rearrange("p (m t b) -> p m t b", t=PACK, b=2),
+        )
+
+        halves = [slice(h * HALF, (h + 1) * HALF) for h in range(J // HALF)]
+        got_s, got_w = [], []
+        for h in range(2):
+            s_h = keep.tile([P, HALF], U8, name=f"got_s{h}", align_bytes=64)
+            nc.vector.tensor_copy(s_h[:], tab_s[:].indirect(offsets[:, h * 32 : (h + 1) * 32]))
+            got_s.append(s_h)
+        for h in range(2):
+            w_h = keep.tile([P, HALF], U32, name=f"got_w{h}", align_bytes=64)
+            nc.vector.tensor_copy(w_h[:], tab_w[:].indirect(offsets[:, h * 32 : (h + 1) * 32]))
+            got_w.append(w_h)
+
+        wg_s = keep.tile([P, N], U8, name="wg_s", align_bytes=64)
+        wh4_s = keep.tile([P, N], U8, name="wh4_s", align_bytes=64)
+        for dst, src in ((wg_s, wg_s_raw), (wh4_s, wh4_s_raw)):
+            nc.vector.tensor_copy(
+                out=dst[:].rearrange("p (t m) -> p m t", t=PACK), in_=src[:].rearrange("p (m t) -> p m t", t=PACK)
+            )
+
+        whd_bf = keep.tile([P, PACK * N], BF16, name="whd_bf", align_bytes=64)
+        nc.scalar.copy(
+            out=whd_bf[:].rearrange("p (t m i) -> p m t i", t=PACK, i=PACK),
+            in_=whd_raw[:].rearrange("p i (m t) -> p m t i", t=PACK),
+        )
+        whd_w = keep.tile([P, N], U32, name="whd_w", align_bytes=64)
+        whd_s = keep.tile([P, N], U8, name="whd_s", align_bytes=64)
+        nc.vector.quantize_mx(out=whd_w[:].bitcast(FP8X4), scales=whd_s[:], in_=whd_bf[:])
+
+        y = keep.tile([P, PACK, J], F32, name="y")
+        y_rows = out_0.rearrange("(p t) j -> t p j", t=PACK)
+        gate, carry, made = [], [], []
+
+        def gates(t):
+            cols = slice(t * P, (t + 1) * P)
+            g_t = keep.tile([P, J], F32, name=f"gate{t}")
+            c_t = keep.tile([P, J], F32, name=f"carry{t}")
+            for h in range(2):
+                ga = psum_g.tile([P, HALF], F32, name="ga")
+                nc.tensor.matmul_mx(
+                    out=ga[:], lhsT=wg_w[:, cols].bitcast(FP8X4), lhsT_scale=wg_s[:, cols],
+                    rhs=got_w[h][:].bitcast(FP8X4), rhs_scale=got_s[h][:], start=True, stop=True,
+                )
+                nc.scalar.activation(g_t[:, halves[h]], ga[:], ACT.Sigmoid, bias=bias[:, t : t + 1])
+            nc.scalar.activation(c_t[:], g_t[:], ACT.Copy, bias=1.0, scale=-1.0)
+            gate.append(g_t)
+            carry.append(c_t)
+
+        def transform(t):
+            cols = slice(t * P, (t + 1) * P)
+            m_t = keep.tile([P, J], F32, name=f"made{t}")
+            for h in range(2):
+                ha = psum_h.tile([P, HALF], F32, name="ha")
+                nc.tensor.matmul_mx(
+                    out=ha[:], lhsT=wh4_w[:, 2 * t * P : 2 * (t + 1) * P].bitcast(FP4X4), lhsT_scale=wh4_s[:, cols],
+                    rhs=got_w[h][:].bitcast(FP8X4), rhs_scale=got_s[h][:], start=True, stop=False,
+                )
+                nc.tensor.matmul_mx(
+                    out=ha[:], lhsT=whd_w[:, cols].bitcast(FP8X4), lhsT_scale=whd_s[:, cols],
+                    rhs=got_w[h][:].bitcast(FP8X4), rhs_scale=got_s[h][:], start=False, stop=True,
+                )
+                nc.vector.scalar_tensor_tensor(
+                    out=m_t[:, halves[h]], in0=ha[:], scalar=0.0, in1=gate[t][:, halves[h]], op0=ALU.max, op1=ALU.mult
+                )
+            made.append(m_t)
+
+        def kept(t, lo, hi):
+            part = ring.tile([P, hi - lo], F32, name="kept")
+            nc.vector.tensor_tensor(part[:], r_tab[t][:].indirect(offsets[:, lo // 16 : hi // 16]), carry[t][:, lo:hi], ALU.mult)
+            return part
+
+        def blend(t, lo, hi, part):
+            nc.vector.tensor_tensor(y[:, t, lo:hi], part[:], made[t][:, lo:hi], ALU.add)
+
+        for t in range(PACK):
+            gates(t)
+        transform(0)
+        transform(1)
+        for t in range(PACK - 1):
+            parts = [kept(t, h * HALF, (h + 1) * HALF) for h in range(2)]
+            for h in range(2):
+                blend(t, h * HALF, (h + 1) * HALF, parts[h])
+            nc.sync.dma_start(out=y_rows[t], in_=y[:, t, :])
+            if t + 2 < PACK:
+                transform(t + 2)
+
+        y_w = keep.tile([P, J], U32, name="y_w", align_bytes=64)
+        y_s = keep.tile([P, J], U8, name="y_s", align_bytes=64)
+        words_out = out_1[0].rearrange("p j i -> p (j i)").bitcast(I32)
+        last = PACK - 1
+        edges = [sum(TAIL[:i]) for i in range(len(TAIL) + 1)]
+        spans = list(zip(edges[:-1], edges[1:]))
+        rounded = []
+
+        def finish(i):
+            lo, hi = spans[i]
+            nc.vector.quantize_mx(out=y_w[:, lo:hi].bitcast(FP8X4), scales=y_s[:, lo:hi], in_=rounded[i][:])
+            if i % 2 == 1:
+                lo2 = spans[i - 1][0]
+                nc.sync.dma_start(out=words_out[:, lo2:hi], in_=y_w[:, lo2:hi].bitcast(I32))
+
+        nxt = kept(last, *spans[0])
+        for i, (lo, hi) in enumerate(spans):
+            cur = nxt
+            if i + 1 < len(spans):
+                nxt = kept(last, *spans[i + 1])
+            blend(last, lo, hi, cur)
+            y_bf = keep.tile([P, (hi - lo) * PACK], BF16, name=f"y_bf{i}", align_bytes=64)
+            nc.scalar.copy(
+                out=y_bf[:].rearrange("p (c i t) -> p c t i", i=4, t=PACK),
+                in_=y[:, :, lo:hi].rearrange("p t (c i) -> p c t i", i=4),
+            )
+            rounded.append(y_bf)
+            if i % 2 == 1:
+                lo2 = spans[i - 1][0]
+                nc.sync.dma_start(out=y_rows[last][:, lo2:hi], in_=y[:, last, lo2:hi])
+            if i >= 1:
+                finish(i - 1)
+        finish(len(spans) - 1)
+        for q in range(4):
+            nc.sync.dma_start(out=out_2[0, 4 * q : 4 * q + 4, :].bitcast(I32), in_=y_s[32 * q : 32 * q + 4, :].bitcast(I32))

@@ -1,6 +1,7 @@
 from contextlib import ExitStack
 
 import concourse.mybir as mybir
+from concourse.masks import make_identity
 
 K, N, T, J = 512, 512, 4096, 1024
 FLOPS = 3 * 2 * K * N * J
@@ -19,11 +20,11 @@ ALU = mybir.AluOpType
 P = 128
 PACK = 4
 HALF = 512
-TAIL = (256, 256, 256, 256)
+TAIL = (256, 256, 256, 128, 128)
 
 
-def load_scale_rows(queue, plane, rows):
-    for q in range(4):
+def load_scale_rows(queue, plane, rows, quadrants):
+    for q in quadrants:
         queue.dma_start(out=plane[32 * q : 32 * q + 4, :].bitcast(I32), in_=rows[0, 4 * q : 4 * q + 4, :].bitcast(I32))
 
 
@@ -34,8 +35,7 @@ def tile_list_hwayt_dl_reluP_kernel(
     with ExitStack() as ctx:
         keep = ctx.enter_context(tc.tile_pool(name="keep", bufs=1))
         ring = ctx.enter_context(tc.tile_pool(name="ring", bufs=2))
-        psum_g = ctx.enter_context(tc.psum_pool(name="psum_g", bufs=3))
-        psum_h = ctx.enter_context(tc.psum_pool(name="psum_h", bufs=5))
+        psum = ctx.enter_context(tc.psum_pool(name="psum", bufs=1))
 
         offsets = keep.tile([P, J // 16], U16, name="offsets")
         nc.sync.dma_start(offsets[:], offs)
@@ -44,27 +44,30 @@ def tile_list_hwayt_dl_reluP_kernel(
         nc.vector.memset(tab_s[:].bitcast(I32), 0)
         wg_s_raw = keep.tile([P, N], U8, name="wg_s_raw", align_bytes=64)
         wh4_s_raw = keep.tile([P, N], U8, name="wh4_s_raw", align_bytes=64)
-        nc.vector.memset(wg_s_raw[:].bitcast(I32), 0)
-        nc.vector.memset(wh4_s_raw[:].bitcast(I32), 0)
+        nc.gpsimd.memset(wg_s_raw[:].bitcast(I32), 0)
+        nc.gpsimd.memset(wh4_s_raw[:].bitcast(I32), 0)
 
         warm = keep.tile([P, 1], F32, name="warm")
         warm2 = keep.tile([P, 1], F32, name="warm2")
-        nc.vector.memset(warm[:], 0.0)
+        nc.gpsimd.memset(warm[:], 0.0)
         nc.scalar.activation(warm2[:], warm[:], ACT.Sigmoid)
+
+        ident = keep.tile([P, P], F32, name="ident")
+        make_identity(nc, ident[:])
 
         wg_raw = keep.tile([P, N], U32, name="wg_raw", align_bytes=64)
         nc.sync.dma_start(out=wg_raw[:].bitcast(I32), in_=wg_words[0].rearrange("p n i -> p (n i)").bitcast(I32))
         wh4_raw = keep.tile([P, 2 * N], U8, name="wh4_raw", align_bytes=64)
         nc.sync.dma_start(out=wh4_raw[:].bitcast(I32), in_=wh4_words[0].bitcast(I32))
-        load_scale_rows(nc.sync, tab_s, tab_scales)
+        load_scale_rows(nc.sync, wg_s_raw, wg_scales, range(4))
         whd_raw = keep.tile([P, PACK, N], F32, name="whd_raw")
         nc.sync.dma_start(out=whd_raw[:], in_=whd.rearrange("(p i) n -> p i n", i=PACK))
-        load_scale_rows(nc.sync, wg_s_raw, wg_scales)
+        load_scale_rows(nc.sync, tab_s, tab_scales, range(4))
         tab_w = keep.tile([P, T], U32, name="tab_w", align_bytes=64)
         nc.sync.dma_start(out=tab_w[:].bitcast(I32), in_=tab_words[0].rearrange("p n i -> p (n i)").bitcast(I32))
         bias = keep.tile([P, PACK], F32, name="bias")
         nc.sync.dma_start(out=bias[:], in_=bg.rearrange("(p t) -> p t", t=PACK))
-        load_scale_rows(nc.sync, wh4_s_raw, wh4_scales)
+        load_scale_rows(nc.sync, wh4_s_raw, wh4_scales, range(4))
         r_rows = rT.rearrange("(p t) c -> t p c", t=PACK)
         r_tab = []
         for t in range(PACK):
@@ -83,24 +86,21 @@ def tile_list_hwayt_dl_reluP_kernel(
             in_=wh4_raw[:].rearrange("p (m t b) -> p m t b", t=PACK, b=2),
         )
 
+        wg_s = keep.tile([P, N], U8, name="wg_s", align_bytes=64)
+        wh4_s = keep.tile([P, N], U8, name="wh4_s", align_bytes=64)
+
+        def deal_scales(dst, src):
+            nc.vector.tensor_copy(
+                out=dst[:].rearrange("p (t m) -> p m t", t=PACK), in_=src[:].rearrange("p (m t) -> p m t", t=PACK)
+            )
+
+        deal_scales(wg_s, wg_s_raw)
         halves = [slice(h * HALF, (h + 1) * HALF) for h in range(J // HALF)]
         got_s, got_w = [], []
         for h in range(2):
             s_h = keep.tile([P, HALF], U8, name=f"got_s{h}", align_bytes=64)
             nc.vector.tensor_copy(s_h[:], tab_s[:].indirect(offsets[:, h * 32 : (h + 1) * 32]))
             got_s.append(s_h)
-        for h in range(2):
-            w_h = keep.tile([P, HALF], U32, name=f"got_w{h}", align_bytes=64)
-            nc.vector.tensor_copy(w_h[:], tab_w[:].indirect(offsets[:, h * 32 : (h + 1) * 32]))
-            got_w.append(w_h)
-
-        wg_s = keep.tile([P, N], U8, name="wg_s", align_bytes=64)
-        wh4_s = keep.tile([P, N], U8, name="wh4_s", align_bytes=64)
-        for dst, src in ((wg_s, wg_s_raw), (wh4_s, wh4_s_raw)):
-            nc.vector.tensor_copy(
-                out=dst[:].rearrange("p (t m) -> p m t", t=PACK), in_=src[:].rearrange("p (m t) -> p m t", t=PACK)
-            )
-
         whd_bf = keep.tile([P, PACK * N], BF16, name="whd_bf", align_bytes=64)
         nc.scalar.copy(
             out=whd_bf[:].rearrange("p (t m i) -> p m t i", t=PACK, i=PACK),
@@ -110,16 +110,22 @@ def tile_list_hwayt_dl_reluP_kernel(
         whd_s = keep.tile([P, N], U8, name="whd_s", align_bytes=64)
         nc.vector.quantize_mx(out=whd_w[:].bitcast(FP8X4), scales=whd_s[:], in_=whd_bf[:])
 
+        for h in range(2):
+            w_h = keep.tile([P, HALF], U32, name=f"got_w{h}", align_bytes=64)
+            nc.vector.tensor_copy(w_h[:], tab_w[:].indirect(offsets[:, h * 32 : (h + 1) * 32]))
+            got_w.append(w_h)
+        deal_scales(wh4_s, wh4_s_raw)
+
         y = keep.tile([P, PACK, J], F32, name="y")
         y_rows = out_0.rearrange("(p t) j -> t p j", t=PACK)
-        gate, carry, made = [], [], []
+        gate, carry, made, sums = [], [], [], []
 
         def gates(t):
             cols = slice(t * P, (t + 1) * P)
-            g_t = keep.tile([P, J], F32, name=f"gate{t}")
+            g_t = keep.tile([P, J], F32, name=f"gate{t}", tag=f"row{t}")
             c_t = keep.tile([P, J], F32, name=f"carry{t}")
             for h in range(2):
-                ga = psum_g.tile([P, HALF], F32, name="ga")
+                ga = psum.tile([P, HALF], F32, name="ga", tag=f"bank{2 * (0, 1, 1, 1)[t] + h}")
                 nc.tensor.matmul_mx(
                     out=ga[:], lhsT=wg_w[:, cols].bitcast(FP8X4), lhsT_scale=wg_s[:, cols],
                     rhs=got_w[h][:].bitcast(FP8X4), rhs_scale=got_s[h][:], start=True, stop=True,
@@ -131,9 +137,8 @@ def tile_list_hwayt_dl_reluP_kernel(
 
         def transform(t):
             cols = slice(t * P, (t + 1) * P)
-            m_t = keep.tile([P, J], F32, name=f"made{t}")
             for h in range(2):
-                ha = psum_h.tile([P, HALF], F32, name="ha")
+                ha = psum.tile([P, HALF], F32, name="ha", tag=f"bank{2 * (1, 2, 3, 0)[t] + h}")
                 nc.tensor.matmul_mx(
                     out=ha[:], lhsT=wh4_w[:, 2 * t * P : 2 * (t + 1) * P].bitcast(FP4X4), lhsT_scale=wh4_s[:, cols],
                     rhs=got_w[h][:].bitcast(FP8X4), rhs_scale=got_s[h][:], start=True, stop=False,
@@ -142,30 +147,56 @@ def tile_list_hwayt_dl_reluP_kernel(
                     out=ha[:], lhsT=whd_w[:, cols].bitcast(FP8X4), lhsT_scale=whd_s[:, cols],
                     rhs=got_w[h][:].bitcast(FP8X4), rhs_scale=got_s[h][:], start=False, stop=True,
                 )
+                sums.append(ha)
+
+        def gated(t):
+            m_t = keep.tile([P, J], F32, name=f"made{t}")
+            for h in range(2):
                 nc.vector.scalar_tensor_tensor(
-                    out=m_t[:, halves[h]], in0=ha[:], scalar=0.0, in1=gate[t][:, halves[h]], op0=ALU.max, op1=ALU.mult
+                    out=m_t[:, halves[h]], in0=sums[2 * t + h][:], scalar=0.0, in1=gate[t][:, halves[h]], op0=ALU.max, op1=ALU.mult
                 )
             made.append(m_t)
 
         def kept(t, lo, hi):
-            part = ring.tile([P, hi - lo], F32, name="kept")
+            tag = f"row{t}" if hi - lo == J else f"tail{lo}"
+            part = keep.tile([P, hi - lo], F32, name=f"kept{t}_{lo}", tag=tag)
             nc.vector.tensor_tensor(part[:], r_tab[t][:].indirect(offsets[:, lo // 16 : hi // 16]), carry[t][:, lo:hi], ALU.mult)
             return part
 
         def blend(t, lo, hi, part):
             nc.vector.tensor_tensor(y[:, t, lo:hi], part[:], made[t][:, lo:hi], ALU.add)
 
-        for t in range(PACK):
-            gates(t)
-        transform(0)
-        transform(1)
-        for t in range(PACK - 1):
-            parts = [kept(t, h * HALF, (h + 1) * HALF) for h in range(2)]
+        def blend_on_tensor(t, part):
+            blocks = [slice(b * P, (b + 1) * P) for b in range(HALF // P)]
+            staged = []
             for h in range(2):
-                blend(t, h * HALF, (h + 1) * HALF, parts[h])
+                turned = psum.tile([P, HALF], F32, name="turned", tag=f"bank{4 + h}")
+                for b in blocks:
+                    nc.tensor.matmul(turned[:, b], made[t][:, halves[h]][:, b], ident[:], start=True, stop=False, is_transpose=True)
+                    nc.tensor.matmul(turned[:, b], part[:, halves[h]][:, b], ident[:], start=False, stop=True, is_transpose=True)
+                s_h = ring.tile([P, HALF], F32, name="staged")
+                nc.scalar.copy(s_h[:], turned[:])
+                staged.append(s_h)
+            for h in range(2):
+                back = psum.tile([P, HALF], F32, name="back", tag=f"bank{2 + h}")
+                for b in blocks:
+                    nc.tensor.transpose(back[:, b], staged[h][:, b], ident[:])
+                nc.scalar.copy(y[:, t, halves[h]], back[:])
             nc.sync.dma_start(out=y_rows[t], in_=y[:, t, :])
-            if t + 2 < PACK:
-                transform(t + 2)
+
+        gates(0)
+        transform(0)
+        gated(0)
+        parts = []
+        for t in range(PACK - 1):
+            gates(t + 1)
+            transform(t + 1)
+            parts.append(kept(t, 0, J))
+            gated(t + 1)
+        blend_on_tensor(0, parts[0])
+        blend_on_tensor(1, parts[1])
+        blend(2, 0, J, parts[2])
+        nc.sync.dma_start(out=y_rows[2], in_=y[:, 2, :])
 
         y_w = keep.tile([P, J], U32, name="y_w", align_bytes=64)
         y_s = keep.tile([P, J], U8, name="y_s", align_bytes=64)
@@ -175,11 +206,13 @@ def tile_list_hwayt_dl_reluP_kernel(
         spans = list(zip(edges[:-1], edges[1:]))
         rounded = []
 
+        stored_after = {1: 0, 2: 2, 4: 3}
+
         def finish(i):
             lo, hi = spans[i]
             nc.vector.quantize_mx(out=y_w[:, lo:hi].bitcast(FP8X4), scales=y_s[:, lo:hi], in_=rounded[i][:])
-            if i % 2 == 1:
-                lo2 = spans[i - 1][0]
+            if i in stored_after:
+                lo2 = spans[stored_after[i]][0]
                 nc.sync.dma_start(out=words_out[:, lo2:hi], in_=y_w[:, lo2:hi].bitcast(I32))
 
         nxt = kept(last, *spans[0])
@@ -188,17 +221,18 @@ def tile_list_hwayt_dl_reluP_kernel(
             if i + 1 < len(spans):
                 nxt = kept(last, *spans[i + 1])
             blend(last, lo, hi, cur)
+            if i in stored_after:
+                lo2 = spans[stored_after[i]][0]
+                nc.sync.dma_start(out=y_rows[last][:, lo2:hi], in_=y[:, last, lo2:hi])
+            if i >= 1:
+                finish(i - 1)
             y_bf = keep.tile([P, (hi - lo) * PACK], BF16, name=f"y_bf{i}", align_bytes=64)
-            nc.scalar.copy(
+            copy = nc.vector.tensor_copy if i == len(spans) - 1 else nc.scalar.copy
+            copy(
                 out=y_bf[:].rearrange("p (c i t) -> p c t i", i=4, t=PACK),
                 in_=y[:, :, lo:hi].rearrange("p t (c i) -> p c t i", i=4),
             )
             rounded.append(y_bf)
-            if i % 2 == 1:
-                lo2 = spans[i - 1][0]
-                nc.sync.dma_start(out=y_rows[last][:, lo2:hi], in_=y[:, last, lo2:hi])
-            if i >= 1:
-                finish(i - 1)
         finish(len(spans) - 1)
         for q in range(4):
-            nc.sync.dma_start(out=out_2[0, 4 * q : 4 * q + 4, :].bitcast(I32), in_=y_s[32 * q : 32 * q + 4, :].bitcast(I32))
+            (nc.sync, nc.scalar)[q % 2].dma_start(out=out_2[0, 4 * q : 4 * q + 4, :].bitcast(I32), in_=y_s[32 * q : 32 * q + 4, :].bitcast(I32))

@@ -47,11 +47,6 @@ def tile_list_hwayt_dl_reluP_kernel(
         nc.gpsimd.memset(wg_s_raw[:].bitcast(I32), 0)
         nc.gpsimd.memset(wh4_s_raw[:].bitcast(I32), 0)
 
-        warm = keep.tile([P, 1], F32, name="warm")
-        warm2 = keep.tile([P, 1], F32, name="warm2")
-        nc.gpsimd.memset(warm[:], 0.0)
-        nc.scalar.activation(warm2[:], warm[:], ACT.Sigmoid)
-
         ident = keep.tile([P, P], F32, name="ident")
         make_identity(nc, ident[:])
 

@@ -23,8 +23,8 @@ HALF = 512
 TAIL = (256, 256, 256, 128, 128)
 
 
-def load_scale_rows(queue, plane, rows, quadrants):
-    for q in quadrants:
+def load_scale_rows(queue, plane, rows):
+    for q in range(4):
         queue.dma_start(out=plane[32 * q : 32 * q + 4, :].bitcast(I32), in_=rows[0, 4 * q : 4 * q + 4, :].bitcast(I32))
 
 
@@ -34,17 +34,17 @@ def tile_list_hwayt_dl_reluP_kernel(
     nc = tc.nc
     with ExitStack() as ctx:
         keep = ctx.enter_context(tc.tile_pool(name="keep", bufs=1))
-        ring = ctx.enter_context(tc.tile_pool(name="ring", bufs=2))
         psum = ctx.enter_context(tc.psum_pool(name="psum", bufs=1))
 
         offsets = keep.tile([P, J // 16], U16, name="offsets")
         nc.sync.dma_start(offsets[:], offs)
 
         tab_s = keep.tile([P, T], U8, name="tab_s", align_bytes=64)
-        nc.vector.memset(tab_s[:].bitcast(I32), 0)
+        nc.vector.memset(tab_s[:, : T // 2].bitcast(I32), 0)
         wg_s_raw = keep.tile([P, N], U8, name="wg_s_raw", align_bytes=64)
-        wh4_s_raw = keep.tile([P, N], U8, name="wh4_s_raw", align_bytes=64)
+        wh4_s_raw = keep.tile([P, N], U8, name="wh4_s_raw", tag="late", align_bytes=64)
         nc.gpsimd.memset(wg_s_raw[:].bitcast(I32), 0)
+        nc.gpsimd.memset(tab_s[:, T // 2 :].bitcast(I32), 0)
         nc.gpsimd.memset(wh4_s_raw[:].bitcast(I32), 0)
 
         ident = keep.tile([P, P], F32, name="ident")
@@ -54,21 +54,24 @@ def tile_list_hwayt_dl_reluP_kernel(
         nc.sync.dma_start(out=wg_raw[:].bitcast(I32), in_=wg_words[0].rearrange("p n i -> p (n i)").bitcast(I32))
         wh4_raw = keep.tile([P, 2 * N], U8, name="wh4_raw", align_bytes=64)
         nc.sync.dma_start(out=wh4_raw[:].bitcast(I32), in_=wh4_words[0].bitcast(I32))
-        load_scale_rows(nc.sync, wg_s_raw, wg_scales, range(4))
+        load_scale_rows(nc.sync, wg_s_raw, wg_scales)
         whd_raw = keep.tile([P, PACK, N], F32, name="whd_raw")
         nc.sync.dma_start(out=whd_raw[:], in_=whd.rearrange("(p i) n -> p i n", i=PACK))
-        load_scale_rows(nc.sync, tab_s, tab_scales, range(4))
+        load_scale_rows(nc.sync, tab_s, tab_scales)
         tab_w = keep.tile([P, T], U32, name="tab_w", align_bytes=64)
         nc.sync.dma_start(out=tab_w[:].bitcast(I32), in_=tab_words[0].rearrange("p n i -> p (n i)").bitcast(I32))
         bias = keep.tile([P, PACK], F32, name="bias")
         nc.sync.dma_start(out=bias[:], in_=bg.rearrange("(p t) -> p t", t=PACK))
-        load_scale_rows(nc.sync, wh4_s_raw, wh4_scales, range(4))
+        load_scale_rows(nc.sync, wh4_s_raw, wh4_scales)
         r_rows = rT.rearrange("(p t) c -> t p c", t=PACK)
         r_tab = []
         for t in range(PACK):
-            r_t = keep.tile([P, T], F32, name=f"r_tab{t}")
+            r_t = keep.tile([P, T], F32, name=f"r_tab{t}", tag=f"r_tab{t}")
             nc.sync.dma_start(out=r_t[:], in_=r_rows[t])
             r_tab.append(r_t)
+
+        neg_bias = keep.tile([P, PACK], F32, name="neg_bias")
+        nc.vector.tensor_scalar(neg_bias[:], bias[:], -1.0, None, ALU.mult)
 
         wg_w = keep.tile([P, N], U32, name="wg_w", align_bytes=64)
         nc.vector.tensor_copy(
@@ -80,7 +83,6 @@ def tile_list_hwayt_dl_reluP_kernel(
             out=wh4_w[:].rearrange("p (t m b) -> p m t b", t=PACK, b=2),
             in_=wh4_raw[:].rearrange("p (m t b) -> p m t b", t=PACK, b=2),
         )
-
         wg_s = keep.tile([P, N], U8, name="wg_s", align_bytes=64)
         wh4_s = keep.tile([P, N], U8, name="wh4_s", align_bytes=64)
 
@@ -96,44 +98,53 @@ def tile_list_hwayt_dl_reluP_kernel(
             s_h = keep.tile([P, HALF], U8, name=f"got_s{h}", align_bytes=64)
             nc.vector.tensor_copy(s_h[:], tab_s[:].indirect(offsets[:, h * 32 : (h + 1) * 32]))
             got_s.append(s_h)
-        whd_bf = keep.tile([P, PACK * N], BF16, name="whd_bf", align_bytes=64)
-        nc.scalar.copy(
-            out=whd_bf[:].rearrange("p (t m i) -> p m t i", t=PACK, i=PACK),
-            in_=whd_raw[:].rearrange("p i (m t) -> p m t i", t=PACK),
-        )
-        whd_w = keep.tile([P, N], U32, name="whd_w", align_bytes=64)
-        whd_s = keep.tile([P, N], U8, name="whd_s", align_bytes=64)
-        nc.vector.quantize_mx(out=whd_w[:].bitcast(FP8X4), scales=whd_s[:], in_=whd_bf[:])
-
         for h in range(2):
-            w_h = keep.tile([P, HALF], U32, name=f"got_w{h}", align_bytes=64)
+            w_h = keep.tile([P, HALF], U32, name=f"got_w{h}", tag=("got_w0", "late")[h], align_bytes=64)
             nc.vector.tensor_copy(w_h[:], tab_w[:].indirect(offsets[:, h * 32 : (h + 1) * 32]))
             got_w.append(w_h)
-        deal_scales(wh4_s, wh4_s_raw)
+            if h == 0:
+                deal_scales(wh4_s, wh4_s_raw)
+        whd_w = keep.tile([P, N], U32, name="whd_w", align_bytes=64)
+        whd_s = keep.tile([P, N], U8, name="whd_s", align_bytes=64)
+        for u, copy in enumerate((nc.scalar.copy, nc.scalar.copy)):
+            whd_bf = keep.tile([P, PACK * N // 2], BF16, name=f"whd_bf{u}", align_bytes=64)
+            copy(
+                out=whd_bf[:].rearrange("p (t m i) -> p m t i", t=2, i=PACK),
+                in_=whd_raw[:].rearrange("p i (m t) -> p m t i", t=PACK)[:, :, 2 * u : 2 * u + 2, :],
+            )
+            cols = slice(u * N // 2, (u + 1) * N // 2)
+            nc.vector.quantize_mx(out=whd_w[:, cols].bitcast(FP8X4), scales=whd_s[:, cols], in_=whd_bf[:])
 
-        y = keep.tile([P, PACK, J], F32, name="y")
+        y_lo = keep.tile([P, 2, J], F32, name="y_lo")
+        y_hi = keep.tile([P, 2, J], F32, name="y_hi")
+        y = [y_lo[:, 0, :], y_lo[:, 1, :], y_hi[:, 0, :], y_hi[:, 1, :]]
         y_rows = out_0.rearrange("(p t) j -> t p j", t=PACK)
-        gate, carry, made, sums = [], [], [], []
+        gate, carry, made, sums, parts = {}, {}, {}, {}, {}
+        on_tensor = (0, 1)
+        blocks = [slice(b * P, (b + 1) * P) for b in range(HALF // P)]
 
         def gates(t):
             cols = slice(t * P, (t + 1) * P)
-            g_t = keep.tile([P, J], F32, name=f"gate{t}", tag=f"row{t}")
-            c_t = keep.tile([P, J], F32, name=f"carry{t}")
+            carry[t] = keep.tile([P, J], F32, name=f"carry{t}", tag=f"carry{t}")
+            if t in on_tensor:
+                gate[t] = keep.tile([P, J], F32, name=f"gate{t}")
             for h in range(2):
-                ga = psum.tile([P, HALF], F32, name="ga", tag=f"bank{2 * (0, 1, 1, 1)[t] + h}")
+                ga = psum.tile([P, HALF], F32, name="ga", tag=f"bank{2 * min(t, 1) + h}")
                 nc.tensor.matmul_mx(
                     out=ga[:], lhsT=wg_w[:, cols].bitcast(FP8X4), lhsT_scale=wg_s[:, cols],
                     rhs=got_w[h][:].bitcast(FP8X4), rhs_scale=got_s[h][:], start=True, stop=True,
                 )
-                nc.scalar.activation(g_t[:, halves[h]], ga[:], ACT.Sigmoid, bias=bias[:, t : t + 1])
-            nc.scalar.activation(c_t[:], g_t[:], ACT.Copy, bias=1.0, scale=-1.0)
-            gate.append(g_t)
-            carry.append(c_t)
+                if t in on_tensor:
+                    nc.scalar.activation(gate[t][:, halves[h]], ga[:], ACT.Sigmoid, bias=bias[:, t : t + 1])
+                else:
+                    nc.scalar.activation(carry[t][:, halves[h]], ga[:], ACT.Sigmoid, bias=neg_bias[:, t : t + 1], scale=-1.0)
+            if t in on_tensor:
+                nc.scalar.activation(carry[t][:], gate[t][:], ACT.Copy, bias=1.0, scale=-1.0)
 
         def transform(t):
             cols = slice(t * P, (t + 1) * P)
             for h in range(2):
-                ha = psum.tile([P, HALF], F32, name="ha", tag=f"bank{2 * (1, 2, 3, 0)[t] + h}")
+                ha = psum.tile([P, HALF], F32, name="ha", tag=f"bank{2 * ((t + 1) % PACK) + h}")
                 nc.tensor.matmul_mx(
                     out=ha[:], lhsT=wh4_w[:, 2 * t * P : 2 * (t + 1) * P].bitcast(FP4X4), lhsT_scale=wh4_s[:, cols],
                     rhs=got_w[h][:].bitcast(FP8X4), rhs_scale=got_s[h][:], start=True, stop=False,
@@ -142,56 +153,65 @@ def tile_list_hwayt_dl_reluP_kernel(
                     out=ha[:], lhsT=whd_w[:, cols].bitcast(FP8X4), lhsT_scale=whd_s[:, cols],
                     rhs=got_w[h][:].bitcast(FP8X4), rhs_scale=got_s[h][:], start=False, stop=True,
                 )
-                sums.append(ha)
+                sums[t, h] = ha
 
         def gated(t):
-            m_t = keep.tile([P, J], F32, name=f"made{t}")
+            made[t] = keep.tile([P, J], F32, name=f"made{t}", tag=("made0", "carry0", "r_tab0", "carry1")[t])
             for h in range(2):
-                nc.vector.scalar_tensor_tensor(
-                    out=m_t[:, halves[h]], in0=sums[2 * t + h][:], scalar=0.0, in1=gate[t][:, halves[h]], op0=ALU.max, op1=ALU.mult
-                )
-            made.append(m_t)
+                if t in on_tensor:
+                    nc.vector.scalar_tensor_tensor(
+                        out=made[t][:, halves[h]], in0=sums[t, h][:], scalar=0.0, in1=gate[t][:, halves[h]], op0=ALU.max, op1=ALU.mult
+                    )
+                else:
+                    nc.vector.scalar_tensor_tensor(
+                        out=made[t][:, halves[h]], in0=carry[t][:, halves[h]], scalar=1.0, in1=sums[t, h][:], op0=ALU.subtract, op1=ALU.mult
+                    )
 
         def kept(t, lo, hi):
-            tag = f"row{t}" if hi - lo == J else f"tail{lo}"
-            part = keep.tile([P, hi - lo], F32, name=f"kept{t}_{lo}", tag=tag)
-            nc.vector.tensor_tensor(part[:], r_tab[t][:].indirect(offsets[:, lo // 16 : hi // 16]), carry[t][:, lo:hi], ALU.mult)
-            return part
+            if lo == 0:
+                parts[t] = keep.tile([P, J], F32, name=f"kept{t}", tag=f"kept{min(t, 2)}")
+            nc.vector.tensor_tensor(parts[t][:, lo:hi], r_tab[t][:].indirect(offsets[:, lo // 16 : hi // 16]), carry[t][:, lo:hi], ALU.mult)
 
-        def blend(t, lo, hi, part):
-            nc.vector.tensor_tensor(y[:, t, lo:hi], part[:], made[t][:, lo:hi], ALU.add)
+        def blend(t, lo, hi):
+            nc.vector.scalar_tensor_tensor(
+                out=y[t][:, lo:hi], in0=made[t][:, lo:hi], scalar=0.0, in1=parts[t][:, lo:hi], op0=ALU.min, op1=ALU.subtract, reverse1=True
+            )
 
-        def blend_on_tensor(t, part):
-            blocks = [slice(b * P, (b + 1) * P) for b in range(HALF // P)]
+        def blend_on_tensor(t):
             staged = []
             for h in range(2):
-                turned = psum.tile([P, HALF], F32, name="turned", tag=f"bank{4 + h}")
+                turned = psum.tile([P, HALF], F32, name="turned", tag=f"bank{2 + h}")
                 for b in blocks:
                     nc.tensor.matmul(turned[:, b], made[t][:, halves[h]][:, b], ident[:], start=True, stop=False, is_transpose=True)
-                    nc.tensor.matmul(turned[:, b], part[:, halves[h]][:, b], ident[:], start=False, stop=True, is_transpose=True)
-                s_h = ring.tile([P, HALF], F32, name="staged")
+                    nc.tensor.matmul(turned[:, b], parts[t][:, halves[h]][:, b], ident[:], start=False, stop=True, is_transpose=True)
+                s_h = keep.tile([P, HALF], F32, name=f"staged{t}_{h}")
                 nc.scalar.copy(s_h[:], turned[:])
                 staged.append(s_h)
             for h in range(2):
-                back = psum.tile([P, HALF], F32, name="back", tag=f"bank{2 + h}")
+                back = psum.tile([P, HALF], F32, name="back", tag=f"bank{4 + 2 * t + h}")
                 for b in blocks:
                     nc.tensor.transpose(back[:, b], staged[h][:, b], ident[:])
-                nc.scalar.copy(y[:, t, halves[h]], back[:])
-            nc.sync.dma_start(out=y_rows[t], in_=y[:, t, :])
+                nc.scalar.copy(y[t][:, halves[h]], back[:])
+            nc.sync.dma_start(out=y_rows[t], in_=y[t])
 
         gates(0)
         transform(0)
         gated(0)
-        parts = []
-        for t in range(PACK - 1):
-            gates(t + 1)
-            transform(t + 1)
-            parts.append(kept(t, 0, J))
-            gated(t + 1)
-        blend_on_tensor(0, parts[0])
-        blend_on_tensor(1, parts[1])
-        blend(2, 0, J, parts[2])
-        nc.sync.dma_start(out=y_rows[2], in_=y[:, 2, :])
+        for t in range(1, PACK):
+            gates(t)
+            transform(t)
+        kept(0, 0, J)
+        gated(1)
+        gated(2)
+        blend_on_tensor(0)
+        kept(1, 0, J)
+        gated(3)
+        blend_on_tensor(1)
+        y_bf = keep.tile([P, J, PACK], BF16, name="y_bf", align_bytes=64)
+        nc.scalar.copy(out=y_bf[:, :, 0:2], in_=y_lo[:].rearrange("p t j -> p j t"))
+        kept(2, 0, J)
+        blend(2, 0, J)
+        nc.sync.dma_start(out=y_rows[2], in_=y[2])
 
         y_w = keep.tile([P, J], U32, name="y_w", align_bytes=64)
         y_s = keep.tile([P, J], U8, name="y_s", align_bytes=64)
@@ -199,35 +219,28 @@ def tile_list_hwayt_dl_reluP_kernel(
         last = PACK - 1
         edges = [sum(TAIL[:i]) for i in range(len(TAIL) + 1)]
         spans = list(zip(edges[:-1], edges[1:]))
-        rounded = []
 
         stored_after = {1: 0, 2: 2, 4: 3}
 
         def finish(i):
             lo, hi = spans[i]
-            nc.vector.quantize_mx(out=y_w[:, lo:hi].bitcast(FP8X4), scales=y_s[:, lo:hi], in_=rounded[i][:])
+            nc.vector.quantize_mx(out=y_w[:, lo:hi].bitcast(FP8X4), scales=y_s[:, lo:hi], in_=y_bf[:, lo:hi, :].rearrange("p j t -> p (j t)"))
             if i in stored_after:
                 lo2 = spans[stored_after[i]][0]
                 nc.sync.dma_start(out=words_out[:, lo2:hi], in_=y_w[:, lo2:hi].bitcast(I32))
 
-        nxt = kept(last, *spans[0])
+        kept(last, *spans[0])
         for i, (lo, hi) in enumerate(spans):
-            cur = nxt
             if i + 1 < len(spans):
-                nxt = kept(last, *spans[i + 1])
-            blend(last, lo, hi, cur)
+                kept(last, *spans[i + 1])
+            blend(last, lo, hi)
             if i in stored_after:
                 lo2 = spans[stored_after[i]][0]
-                nc.sync.dma_start(out=y_rows[last][:, lo2:hi], in_=y[:, last, lo2:hi])
+                nc.sync.dma_start(out=y_rows[last][:, lo2:hi], in_=y[last][:, lo2:hi])
             if i >= 1:
                 finish(i - 1)
-            y_bf = keep.tile([P, (hi - lo) * PACK], BF16, name=f"y_bf{i}", align_bytes=64)
             copy = nc.vector.tensor_copy if i == len(spans) - 1 else nc.scalar.copy
-            copy(
-                out=y_bf[:].rearrange("p (c i t) -> p c t i", i=4, t=PACK),
-                in_=y[:, :, lo:hi].rearrange("p t (c i) -> p c t i", i=4),
-            )
-            rounded.append(y_bf)
+            copy(out=y_bf[:, lo:hi, 2:4], in_=y_hi[:, :, lo:hi].rearrange("p t j -> p j t"))
         finish(len(spans) - 1)
         for q in range(4):
             (nc.sync, nc.scalar)[q % 2].dma_start(out=out_2[0, 4 * q : 4 * q + 4, :].bitcast(I32), in_=y_s[32 * q : 32 * q + 4, :].bitcast(I32))

@@ -120,7 +120,7 @@ def tile_list_hwayt_dl_reluP_kernel(
         y = [y_lo[:, 0, :], y_lo[:, 1, :], y_hi[:, 0, :], y_hi[:, 1, :]]
         y_rows = out_0.rearrange("(p t) j -> t p j", t=PACK)
         gate, carry, made, sums, parts = {}, {}, {}, {}, {}
-        on_tensor = (0, 1)
+        on_tensor = (0,)
         blocks = [slice(b * P, (b + 1) * P) for b in range(HALF // P)]
 
         def gates(t):
@@ -206,7 +206,8 @@ def tile_list_hwayt_dl_reluP_kernel(
         blend_on_tensor(0)
         kept(1, 0, J)
         gated(3)
-        blend_on_tensor(1)
+        blend(1, 0, J)
+        nc.sync.dma_start(out=y_rows[1], in_=y[1])
         y_bf = keep.tile([P, J, PACK], BF16, name="y_bf", align_bytes=64)
         nc.scalar.copy(out=y_bf[:, :, 0:2], in_=y_lo[:].rearrange("p t j -> p j t"))
         kept(2, 0, J)

@@ -120,7 +120,7 @@ def tile_list_hwayt_dl_reluP_kernel(
         y = [y_lo[:, 0, :], y_lo[:, 1, :], y_hi[:, 0, :], y_hi[:, 1, :]]
         y_rows = out_0.rearrange("(p t) j -> t p j", t=PACK)
         gate, carry, made, sums, parts = {}, {}, {}, {}, {}
-        on_tensor = (0,)
+        on_tensor = (0, 1)
         blocks = [slice(b * P, (b + 1) * P) for b in range(HALF // P)]
 
         def gates(t):
@@ -156,7 +156,7 @@ def tile_list_hwayt_dl_reluP_kernel(
                 sums[t, h] = ha
 
         def gated(t):
-            made[t] = keep.tile([P, J], F32, name=f"made{t}", tag=("made0", "carry0", "r_tab0", "carry1")[t])
+            made[t] = keep.tile([P, J], F32, name=f"made{t}", tag=("made0", "carry0", "carry1", "r_tab1")[t])
             for h in range(2):
                 if t in on_tensor:
                     nc.vector.scalar_tensor_tensor(
@@ -202,11 +202,11 @@ def tile_list_hwayt_dl_reluP_kernel(
             transform(t)
         kept(0, 0, J)
         gated(1)
-        gated(2)
         blend_on_tensor(0)
         kept(1, 0, J)
+        gated(2)
         gated(3)
-        blend(1, 0, J)
+        nc.gpsimd.tensor_tensor(y[1], parts[1][:], made[1][:], ALU.add)
         nc.sync.dma_start(out=y_rows[1], in_=y[1])
         y_bf = keep.tile([P, J, PACK], BF16, name="y_bf", align_bytes=64)
         nc.scalar.copy(out=y_bf[:, :, 0:2], in_=y_lo[:].rearrange("p t j -> p j t"))

@@ -24,8 +24,8 @@ TAIL = (256, 256, 256, 128, 128)
 
 
 def load_scale_rows(queue, plane, rows):
-    for q in range(4):
-        queue.dma_start(out=plane[32 * q : 32 * q + 4, :].bitcast(I32), in_=rows[0, 4 * q : 4 * q + 4, :].bitcast(I32))
+    for r in range(4):
+        queue.dma_start(out=plane[r:P:32, :].bitcast(I32), in_=rows[0, r:16:4, :].bitcast(I32))
 
 
 def tile_list_hwayt_dl_reluP_kernel(
@@ -243,5 +243,5 @@ def tile_list_hwayt_dl_reluP_kernel(
             copy = nc.vector.tensor_copy if i == len(spans) - 1 else nc.scalar.copy
             copy(out=y_bf[:, lo:hi, 2:4], in_=y_hi[:, :, lo:hi].rearrange("p t j -> p j t"))
         finish(len(spans) - 1)
-        for q in range(4):
-            (nc.sync, nc.scalar)[q % 2].dma_start(out=out_2[0, 4 * q : 4 * q + 4, :].bitcast(I32), in_=y_s[32 * q : 32 * q + 4, :].bitcast(I32))
+        for r in range(4):
+            (nc.sync, nc.scalar)[r % 2].dma_start(out=out_2[0, r:16:4, :].bitcast(I32), in_=y_s[r:P:32, :].bitcast(I32))

@@ -120,7 +120,7 @@ def tile_list_hwayt_dl_reluP_kernel(
         y = [y_lo[:, 0, :], y_lo[:, 1, :], y_hi[:, 0, :], y_hi[:, 1, :]]
         y_rows = out_0.rearrange("(p t) j -> t p j", t=PACK)
         gate, carry, made, sums, parts = {}, {}, {}, {}, {}
-        on_tensor = (0, 1)
+        on_tensor = (0, 1, 2)
         blocks = [slice(b * P, (b + 1) * P) for b in range(HALF // P)]
 
         def gates(t):
@@ -156,7 +156,7 @@ def tile_list_hwayt_dl_reluP_kernel(
                 sums[t, h] = ha
 
         def gated(t):
-            made[t] = keep.tile([P, J], F32, name=f"made{t}", tag=("made0", "carry0", "carry1", "r_tab1")[t])
+            made[t] = keep.tile([P, J], F32, name=f"made{t}", tag=("made0", "carry0", "carry1", "carry2")[t])
             for h in range(2):
                 if t in on_tensor:
                     nc.vector.scalar_tensor_tensor(
@@ -177,22 +177,17 @@ def tile_list_hwayt_dl_reluP_kernel(
                 out=y[t][:, lo:hi], in0=made[t][:, lo:hi], scalar=0.0, in1=parts[t][:, lo:hi], op0=ALU.min, op1=ALU.subtract, reverse1=True
             )
 
-        def blend_on_tensor(t):
-            staged = []
-            for h in range(2):
-                turned = psum.tile([P, HALF], F32, name="turned", tag=f"bank{2 + h}")
-                for b in blocks:
-                    nc.tensor.matmul(turned[:, b], made[t][:, halves[h]][:, b], ident[:], start=True, stop=False, is_transpose=True)
-                    nc.tensor.matmul(turned[:, b], parts[t][:, halves[h]][:, b], ident[:], start=False, stop=True, is_transpose=True)
-                s_h = keep.tile([P, HALF], F32, name=f"staged{t}_{h}")
-                nc.scalar.copy(s_h[:], turned[:])
-                staged.append(s_h)
-            for h in range(2):
-                back = psum.tile([P, HALF], F32, name="back", tag=f"bank{4 + 2 * t + h}")
-                for b in blocks:
-                    nc.tensor.transpose(back[:, b], staged[h][:, b], ident[:])
-                nc.scalar.copy(y[t][:, halves[h]], back[:])
-            nc.sync.dma_start(out=y_rows[t], in_=y[t])
+        def blend_on_tensor(t, half):
+            turned = psum.tile([P, HALF], F32, name="turned", tag="bank2")
+            for b in blocks:
+                nc.tensor.matmul(turned[:, b], made[t][:, half][:, b], ident[:], start=True, stop=False, is_transpose=True)
+                nc.tensor.matmul(turned[:, b], parts[t][:, half][:, b], ident[:], start=False, stop=True, is_transpose=True)
+            staged = keep.tile([P, HALF], F32, name=f"staged{t}")
+            nc.scalar.copy(staged[:], turned[:])
+            back = psum.tile([P, HALF], F32, name="back", tag="bank3")
+            for b in blocks:
+                nc.tensor.transpose(back[:, b], staged[:, b], ident[:])
+            nc.scalar.copy(y[t][:, half], back[:])
 
         gates(0)
         transform(0)
@@ -200,19 +195,19 @@ def tile_list_hwayt_dl_reluP_kernel(
         for t in range(1, PACK):
             gates(t)
             transform(t)
-        kept(0, 0, J)
-        gated(1)
-        blend_on_tensor(0)
-        kept(1, 0, J)
-        gated(2)
-        gated(3)
-        nc.gpsimd.tensor_tensor(y[1], parts[1][:], made[1][:], ALU.add)
-        nc.sync.dma_start(out=y_rows[1], in_=y[1])
         y_bf = keep.tile([P, J, PACK], BF16, name="y_bf", align_bytes=64)
-        nc.scalar.copy(out=y_bf[:, :, 0:2], in_=y_lo[:].rearrange("p t j -> p j t"))
-        kept(2, 0, J)
-        blend(2, 0, J)
-        nc.sync.dma_start(out=y_rows[2], in_=y[2])
+        first, second = halves
+        for t in range(PACK - 1):
+            kept(t, 0, J)
+            gated(t + 1)
+            nc.gpsimd.tensor_tensor(y[t][:, first], parts[t][:, first], made[t][:, first], ALU.add)
+            if t < 2:
+                blend_on_tensor(t, second)
+            else:
+                nc.vector.tensor_tensor(y[t][:, second], parts[t][:, second], made[t][:, second], ALU.add)
+            nc.sync.dma_start(out=y_rows[t], in_=y[t])
+            if t == 1:
+                nc.scalar.copy(out=y_bf[:, :, 0:2], in_=y_lo[:].rearrange("p t j -> p j t"))
 
         y_w = keep.tile([P, J], U32, name="y_w", align_bytes=64)
         y_s = keep.tile([P, J], U8, name="y_s", align_bytes=64)

@@ -123,49 +123,50 @@ def tile_list_hwayt_dl_reluP_kernel(
         on_tensor = (0, 1, 2)
         blocks = [slice(b * P, (b + 1) * P) for b in range(HALF // P)]
 
-        def gates(t):
+        def gates(t, h):
             cols = slice(t * P, (t + 1) * P)
-            carry[t] = keep.tile([P, J], F32, name=f"carry{t}", tag=f"carry{t}")
-            if t in on_tensor:
-                gate[t] = keep.tile([P, J], F32, name=f"gate{t}")
-            for h in range(2):
-                ga = psum.tile([P, HALF], F32, name="ga", tag=f"bank{2 * min(t, 1) + h}")
-                nc.tensor.matmul_mx(
-                    out=ga[:], lhsT=wg_w[:, cols].bitcast(FP8X4), lhsT_scale=wg_s[:, cols],
-                    rhs=got_w[h][:].bitcast(FP8X4), rhs_scale=got_s[h][:], start=True, stop=True,
-                )
+            if h == 0:
+                carry[t] = keep.tile([P, J], F32, name=f"carry{t}", tag=f"carry{t}")
                 if t in on_tensor:
-                    nc.scalar.activation(gate[t][:, halves[h]], ga[:], ACT.Sigmoid, bias=bias[:, t : t + 1])
-                else:
-                    nc.scalar.activation(carry[t][:, halves[h]], ga[:], ACT.Sigmoid, bias=neg_bias[:, t : t + 1], scale=-1.0)
+                    gate[t] = keep.tile([P, J], F32, name=f"gate{t}")
+            ga = psum.tile([P, HALF], F32, name="ga", tag=f"bank{(2 * min(t, 1), 1)[h]}")
+            nc.tensor.matmul_mx(
+                out=ga[:], lhsT=wg_w[:, cols].bitcast(FP8X4), lhsT_scale=wg_s[:, cols],
+                rhs=got_w[h][:].bitcast(FP8X4), rhs_scale=got_s[h][:], start=True, stop=True,
+            )
+            reads = [(carry[t], neg_bias, -1.0)]
             if t in on_tensor:
-                nc.scalar.activation(carry[t][:], gate[t][:], ACT.Copy, bias=1.0, scale=-1.0)
+                reads.insert(int((t, h) == (0, 1)), (gate[t], bias, 1.0))
+            for dst, offset, sign in reads:
+                nc.scalar.activation(dst[:, halves[h]], ga[:], ACT.Sigmoid, bias=offset[:, t : t + 1], scale=sign)
 
-        def transform(t):
+        def transform(t, h):
             cols = slice(t * P, (t + 1) * P)
-            for h in range(2):
-                ha = psum.tile([P, HALF], F32, name="ha", tag=f"bank{2 * ((t + 1) % PACK) + h}")
-                nc.tensor.matmul_mx(
-                    out=ha[:], lhsT=wh4_w[:, 2 * t * P : 2 * (t + 1) * P].bitcast(FP4X4), lhsT_scale=wh4_s[:, cols],
-                    rhs=got_w[h][:].bitcast(FP8X4), rhs_scale=got_s[h][:], start=True, stop=False,
-                )
-                nc.tensor.matmul_mx(
-                    out=ha[:], lhsT=whd_w[:, cols].bitcast(FP8X4), lhsT_scale=whd_s[:, cols],
-                    rhs=got_w[h][:].bitcast(FP8X4), rhs_scale=got_s[h][:], start=False, stop=True,
-                )
-                sums[t, h] = ha
+            ha = psum.tile([P, HALF], F32, name="ha", tag=f"bank{((2, 3), (4, 5), (6, 7), (0, 3))[t][h]}")
+            nc.tensor.matmul_mx(
+                out=ha[:], lhsT=wh4_w[:, 2 * t * P : 2 * (t + 1) * P].bitcast(FP4X4), lhsT_scale=wh4_s[:, cols],
+                rhs=got_w[h][:].bitcast(FP8X4), rhs_scale=got_s[h][:], start=True, stop=False,
+            )
+            nc.tensor.matmul_mx(
+                out=ha[:], lhsT=whd_w[:, cols].bitcast(FP8X4), lhsT_scale=whd_s[:, cols],
+                rhs=got_w[h][:].bitcast(FP8X4), rhs_scale=got_s[h][:], start=False, stop=True,
+            )
+            sums[t, h] = ha
 
-        def gated(t):
-            made[t] = keep.tile([P, J], F32, name=f"made{t}", tag=("made0", "carry0", "carry1", "carry2")[t])
-            for h in range(2):
-                if t in on_tensor:
-                    nc.vector.scalar_tensor_tensor(
-                        out=made[t][:, halves[h]], in0=sums[t, h][:], scalar=0.0, in1=gate[t][:, halves[h]], op0=ALU.max, op1=ALU.mult
-                    )
-                else:
-                    nc.vector.scalar_tensor_tensor(
-                        out=made[t][:, halves[h]], in0=carry[t][:, halves[h]], scalar=1.0, in1=sums[t, h][:], op0=ALU.subtract, op1=ALU.mult
-                    )
+        def gated(t, h):
+            behind = {(0, 0): "made00", (0, 1): "r_tab0", (1, 0): "carry0", (2, 0): "carry1", (3, 0): "carry2"}
+            if (t, h) in behind:
+                made[t, h] = keep.tile([P, J], F32, name=f"made{t}_{h}", tag=behind[t, h])
+            else:
+                made[t, h] = made[t, 0]
+            if t in on_tensor:
+                nc.vector.scalar_tensor_tensor(
+                    out=made[t, h][:, halves[h]], in0=sums[t, h][:], scalar=0.0, in1=gate[t][:, halves[h]], op0=ALU.max, op1=ALU.mult
+                )
+            else:
+                nc.vector.scalar_tensor_tensor(
+                    out=made[t, h][:, halves[h]], in0=carry[t][:, halves[h]], scalar=1.0, in1=sums[t, h][:], op0=ALU.subtract, op1=ALU.mult
+                )
 
         def kept(t, lo, hi):
             if lo == 0:
@@ -174,37 +175,46 @@ def tile_list_hwayt_dl_reluP_kernel(
 
         def blend(t, lo, hi):
             nc.vector.scalar_tensor_tensor(
-                out=y[t][:, lo:hi], in0=made[t][:, lo:hi], scalar=0.0, in1=parts[t][:, lo:hi], op0=ALU.min, op1=ALU.subtract, reverse1=True
+                out=y[t][:, lo:hi], in0=made[t, 0][:, lo:hi], scalar=0.0, in1=parts[t][:, lo:hi], op0=ALU.min, op1=ALU.subtract, reverse1=True
             )
 
         def blend_on_tensor(t, half):
             turned = psum.tile([P, HALF], F32, name="turned", tag="bank2")
             for b in blocks:
-                nc.tensor.matmul(turned[:, b], made[t][:, half][:, b], ident[:], start=True, stop=False, is_transpose=True)
+                nc.tensor.matmul(turned[:, b], made[t, 1][:, half][:, b], ident[:], start=True, stop=False, is_transpose=True)
                 nc.tensor.matmul(turned[:, b], parts[t][:, half][:, b], ident[:], start=False, stop=True, is_transpose=True)
             staged = keep.tile([P, HALF], F32, name=f"staged{t}")
             nc.scalar.copy(staged[:], turned[:])
-            back = psum.tile([P, HALF], F32, name="back", tag="bank3")
+            back = psum.tile([P, HALF], F32, name="back", tag="bank1")
             for b in blocks:
                 nc.tensor.transpose(back[:, b], staged[:, b], ident[:])
             nc.scalar.copy(y[t][:, half], back[:])
 
-        gates(0)
-        transform(0)
-        gated(0)
+        for h in range(2):
+            gates(0, h)
+            transform(0, h)
+        gated(0, 0)
         for t in range(1, PACK):
-            gates(t)
-            transform(t)
+            for h in range(2):
+                gates(t, h)
+            if t < 3:
+                for h in range(2):
+                    transform(t, h)
         y_bf = keep.tile([P, J, PACK], BF16, name="y_bf", align_bytes=64)
         first, second = halves
         for t in range(PACK - 1):
             kept(t, 0, J)
-            gated(t + 1)
-            nc.gpsimd.tensor_tensor(y[t][:, first], parts[t][:, first], made[t][:, first], ALU.add)
+            if t == 0:
+                gated(0, 1)
+                for h in range(2):
+                    transform(3, h)
+            for h in range(2):
+                gated(t + 1, h)
+            nc.gpsimd.tensor_tensor(y[t][:, first], parts[t][:, first], made[t, 0][:, first], ALU.add)
             if t < 2:
                 blend_on_tensor(t, second)
             else:
-                nc.vector.tensor_tensor(y[t][:, second], parts[t][:, second], made[t][:, second], ALU.add)
+                nc.vector.tensor_tensor(y[t][:, second], parts[t][:, second], made[t, 1][:, second], ALU.add)
             nc.sync.dma_start(out=y_rows[t], in_=y[t])
             if t == 1:
                 nc.scalar.copy(out=y_bf[:, :, 0:2], in_=y_lo[:].rearrange("p t j -> p j t"))

@@ -20,6 +20,7 @@ ALU = mybir.AluOpType
 P = 128
 PACK = 4
 HALF = 512
+SHARE = 768
 TAIL = (256, 256, 256, 128, 128)
 
 
@@ -55,14 +56,16 @@ def tile_list_hwayt_dl_reluP_kernel(
         wh4_raw = keep.tile([P, 2 * N], U8, name="wh4_raw", align_bytes=64)
         nc.sync.dma_start(out=wh4_raw[:].bitcast(I32), in_=wh4_words[0].bitcast(I32))
         load_scale_rows(nc.sync, wg_s_raw, wg_scales)
-        whd_raw = keep.tile([P, PACK, N], F32, name="whd_raw")
-        nc.sync.dma_start(out=whd_raw[:], in_=whd.rearrange("(p i) n -> p i n", i=PACK))
-        load_scale_rows(nc.sync, tab_s, tab_scales)
         tab_w = keep.tile([P, T], U32, name="tab_w", align_bytes=64)
-        nc.sync.dma_start(out=tab_w[:].bitcast(I32), in_=tab_words[0].rearrange("p n i -> p (n i)").bitcast(I32))
+        tab_rows = tab_words[0].rearrange("p n i -> p (n i)").bitcast(I32)
+        nc.sync.dma_start(out=tab_w[:, : T // 2].bitcast(I32), in_=tab_rows[:, : T // 2])
+        load_scale_rows(nc.sync, tab_s, tab_scales)
+        nc.sync.dma_start(out=tab_w[:, T // 2 :].bitcast(I32), in_=tab_rows[:, T // 2 :])
         bias = keep.tile([P, PACK], F32, name="bias")
         nc.sync.dma_start(out=bias[:], in_=bg.rearrange("(p t) -> p t", t=PACK))
         load_scale_rows(nc.sync, wh4_s_raw, wh4_scales)
+        whd_raw = keep.tile([P, PACK, N], F32, name="whd_raw")
+        nc.sync.dma_start(out=whd_raw[:], in_=whd.rearrange("(p i) n -> p i n", i=PACK))
         r_rows = rT.rearrange("(p t) c -> t p c", t=PACK)
         r_tab = []
         for t in range(PACK):
@@ -106,7 +109,7 @@ def tile_list_hwayt_dl_reluP_kernel(
                 deal_scales(wh4_s, wh4_s_raw)
         whd_w = keep.tile([P, N], U32, name="whd_w", align_bytes=64)
         whd_s = keep.tile([P, N], U8, name="whd_s", align_bytes=64)
-        for u, copy in enumerate((nc.scalar.copy, nc.scalar.copy)):
+        for u, copy in enumerate((nc.vector.tensor_copy, nc.vector.tensor_copy)):
             whd_bf = keep.tile([P, PACK * N // 2], BF16, name=f"whd_bf{u}", align_bytes=64)
             copy(
                 out=whd_bf[:].rearrange("p (t m i) -> p m t i", t=2, i=PACK),
@@ -120,8 +123,8 @@ def tile_list_hwayt_dl_reluP_kernel(
         y = [y_lo[:, 0, :], y_lo[:, 1, :], y_hi[:, 0, :], y_hi[:, 1, :]]
         y_rows = out_0.rearrange("(p t) j -> t p j", t=PACK)
         gate, carry, made, sums, parts = {}, {}, {}, {}, {}
-        on_tensor = (0, 1, 2)
-        blocks = [slice(b * P, (b + 1) * P) for b in range(HALF // P)]
+        on_tensor = (0, 1)
+        blocks = [slice(b * P, (b + 1) * P) for b in range((J - SHARE) // P)]
 
         def gates(t, h):
             cols = slice(t * P, (t + 1) * P)
@@ -129,7 +132,7 @@ def tile_list_hwayt_dl_reluP_kernel(
                 carry[t] = keep.tile([P, J], F32, name=f"carry{t}", tag=f"carry{t}")
                 if t in on_tensor:
                     gate[t] = keep.tile([P, J], F32, name=f"gate{t}")
-            ga = psum.tile([P, HALF], F32, name="ga", tag=f"bank{(2 * min(t, 1), 1)[h]}")
+            ga = psum.tile([P, HALF], F32, name="ga", tag=f"bank{2 * min(t, 1) + h}")
             nc.tensor.matmul_mx(
                 out=ga[:], lhsT=wg_w[:, cols].bitcast(FP8X4), lhsT_scale=wg_s[:, cols],
                 rhs=got_w[h][:].bitcast(FP8X4), rhs_scale=got_s[h][:], start=True, stop=True,
@@ -142,19 +145,22 @@ def tile_list_hwayt_dl_reluP_kernel(
 
         def transform(t, h):
             cols = slice(t * P, (t + 1) * P)
-            ha = psum.tile([P, HALF], F32, name="ha", tag=f"bank{((2, 3), (4, 5), (6, 7), (0, 3))[t][h]}")
-            nc.tensor.matmul_mx(
-                out=ha[:], lhsT=wh4_w[:, 2 * t * P : 2 * (t + 1) * P].bitcast(FP4X4), lhsT_scale=wh4_s[:, cols],
-                rhs=got_w[h][:].bitcast(FP8X4), rhs_scale=got_s[h][:], start=True, stop=False,
-            )
-            nc.tensor.matmul_mx(
-                out=ha[:], lhsT=whd_w[:, cols].bitcast(FP8X4), lhsT_scale=whd_s[:, cols],
-                rhs=got_w[h][:].bitcast(FP8X4), rhs_scale=got_s[h][:], start=False, stop=True,
-            )
+            ha = psum.tile([P, HALF], F32, name="ha", tag=f"bank{2 * ((t + 1) % PACK) + h}")
+            passes = [
+                (wh4_w[:, 2 * t * P : 2 * (t + 1) * P].bitcast(FP4X4), wh4_s[:, cols]),
+                (whd_w[:, cols].bitcast(FP8X4), whd_s[:, cols]),
+            ]
+            if t > 0:
+                passes = passes[::-1]
+            for i, (codes, scales) in enumerate(passes):
+                nc.tensor.matmul_mx(
+                    out=ha[:], lhsT=codes, lhsT_scale=scales,
+                    rhs=got_w[h][:].bitcast(FP8X4), rhs_scale=got_s[h][:], start=i == 0, stop=i == 1,
+                )
             sums[t, h] = ha
 
         def gated(t, h):
-            behind = {(0, 0): "made00", (0, 1): "r_tab0", (1, 0): "carry0", (2, 0): "carry1", (3, 0): "carry2"}
+            behind = {(0, 0): "made00", (1, 0): "carry0", (2, 0): "r_tab0", (2, 1): "carry1", (3, 0): "r_tab1"}
             if (t, h) in behind:
                 made[t, h] = keep.tile([P, J], F32, name=f"made{t}_{h}", tag=behind[t, h])
             else:
@@ -175,17 +181,17 @@ def tile_list_hwayt_dl_reluP_kernel(
 
         def blend(t, lo, hi):
             nc.vector.scalar_tensor_tensor(
-                out=y[t][:, lo:hi], in0=made[t, 0][:, lo:hi], scalar=0.0, in1=parts[t][:, lo:hi], op0=ALU.min, op1=ALU.subtract, reverse1=True
+                out=y[t][:, lo:hi], in0=made[t, lo // HALF][:, lo:hi], scalar=0.0, in1=parts[t][:, lo:hi], op0=ALU.min, op1=ALU.subtract, reverse1=True
             )
 
         def blend_on_tensor(t, half):
-            turned = psum.tile([P, HALF], F32, name="turned", tag="bank2")
+            turned = psum.tile([P, J - SHARE], F32, name="turned", tag="bank2")
             for b in blocks:
                 nc.tensor.matmul(turned[:, b], made[t, 1][:, half][:, b], ident[:], start=True, stop=False, is_transpose=True)
                 nc.tensor.matmul(turned[:, b], parts[t][:, half][:, b], ident[:], start=False, stop=True, is_transpose=True)
-            staged = keep.tile([P, HALF], F32, name=f"staged{t}")
+            staged = keep.tile([P, J - SHARE], F32, name=f"staged{t}")
             nc.scalar.copy(staged[:], turned[:])
-            back = psum.tile([P, HALF], F32, name="back", tag="bank1")
+            back = psum.tile([P, J - SHARE], F32, name="back", tag="bank3")
             for b in blocks:
                 nc.tensor.transpose(back[:, b], staged[:, b], ident[:])
             nc.scalar.copy(y[t][:, half], back[:])
@@ -193,31 +199,35 @@ def tile_list_hwayt_dl_reluP_kernel(
         for h in range(2):
             gates(0, h)
             transform(0, h)
-        gated(0, 0)
+        for h in range(2):
+            gated(0, h)
         for t in range(1, PACK):
             for h in range(2):
                 gates(t, h)
-            if t < 3:
-                for h in range(2):
-                    transform(t, h)
+            for h in range(2):
+                transform(t, h)
         y_bf = keep.tile([P, J, PACK], BF16, name="y_bf", align_bytes=64)
-        first, second = halves
+        first, second = slice(0, SHARE), slice(SHARE, J)
+
+        def round_early(half):
+            nc.scalar.copy(out=y_bf[:, half, 0:2], in_=y_lo[:, :, half].rearrange("p t j -> p j t"))
+
+        behind_gather = (((1, 0), (1, 1), (2, 0)), ((2, 1), (3, 0), (3, 1)), ())
         for t in range(PACK - 1):
             kept(t, 0, J)
-            if t == 0:
-                gated(0, 1)
-                for h in range(2):
-                    transform(3, h)
-            for h in range(2):
-                gated(t + 1, h)
-            nc.gpsimd.tensor_tensor(y[t][:, first], parts[t][:, first], made[t, 0][:, first], ALU.add)
+            for u, h in behind_gather[t]:
+                gated(u, h)
             if t < 2:
+                nc.gpsimd.tensor_tensor(y[t][:, first], parts[t][:, first], made[t, 0][:, first], ALU.add)
+                if t == 1:
+                    round_early(first)
                 blend_on_tensor(t, second)
+                if t == 1:
+                    round_early(second)
             else:
-                nc.vector.tensor_tensor(y[t][:, second], parts[t][:, second], made[t, 1][:, second], ALU.add)
+                blend(t, 0, HALF)
+                blend(t, HALF, J)
             nc.sync.dma_start(out=y_rows[t], in_=y[t])
-            if t == 1:
-                nc.scalar.copy(out=y_bf[:, :, 0:2], in_=y_lo[:].rearrange("p t j -> p j t"))
 
         y_w = keep.tile([P, J], U32, name="y_w", align_bytes=64)
         y_s = keep.tile([P, J], U8, name="y_s", align_bytes=64)

@@ -21,7 +21,7 @@ P = 128
 PACK = 4
 HALF = 512
 SHARE = 768
-TAIL = (256, 256, 256, 128, 128)
+TAIL = (256, 256, 256, 256)
 
 
 def load_scale_rows(queue, plane, rows):
@@ -123,14 +123,13 @@ def tile_list_hwayt_dl_reluP_kernel(
         y = [y_lo[:, 0, :], y_lo[:, 1, :], y_hi[:, 0, :], y_hi[:, 1, :]]
         y_rows = out_0.rearrange("(p t) j -> t p j", t=PACK)
         gate, carry, made, sums, parts = {}, {}, {}, {}, {}
-        on_tensor = (0, 1)
-        blocks = [slice(b * P, (b + 1) * P) for b in range((J - SHARE) // P)]
+        on_tensor = ((0, 0), (0, 1), (1, 0), (1, 1), (2, 0))
 
         def gates(t, h):
             cols = slice(t * P, (t + 1) * P)
             if h == 0:
                 carry[t] = keep.tile([P, J], F32, name=f"carry{t}", tag=f"carry{t}")
-                if t in on_tensor:
+                if (t, h) in on_tensor:
                     gate[t] = keep.tile([P, J], F32, name=f"gate{t}")
             ga = psum.tile([P, HALF], F32, name="ga", tag=f"bank{2 * min(t, 1) + h}")
             nc.tensor.matmul_mx(
@@ -138,7 +137,7 @@ def tile_list_hwayt_dl_reluP_kernel(
                 rhs=got_w[h][:].bitcast(FP8X4), rhs_scale=got_s[h][:], start=True, stop=True,
             )
             reads = [(carry[t], neg_bias, -1.0)]
-            if t in on_tensor:
+            if (t, h) in on_tensor:
                 reads.insert(int((t, h) == (0, 1)), (gate[t], bias, 1.0))
             for dst, offset, sign in reads:
                 nc.scalar.activation(dst[:, halves[h]], ga[:], ACT.Sigmoid, bias=offset[:, t : t + 1], scale=sign)
@@ -165,7 +164,7 @@ def tile_list_hwayt_dl_reluP_kernel(
                 made[t, h] = keep.tile([P, J], F32, name=f"made{t}_{h}", tag=behind[t, h])
             else:
                 made[t, h] = made[t, 0]
-            if t in on_tensor:
+            if (t, h) in on_tensor:
                 nc.vector.scalar_tensor_tensor(
                     out=made[t, h][:, halves[h]], in0=sums[t, h][:], scalar=0.0, in1=gate[t][:, halves[h]], op0=ALU.max, op1=ALU.mult
                 )
@@ -176,7 +175,7 @@ def tile_list_hwayt_dl_reluP_kernel(
 
         def kept(t, lo, hi):
             if lo == 0:
-                parts[t] = keep.tile([P, J], F32, name=f"kept{t}", tag=f"kept{min(t, 2)}")
+                parts[t] = keep.tile([P, J], F32, name=f"kept{t}", tag=("kept0", "kept1", "kept2", "carry1")[t])
             nc.vector.tensor_tensor(parts[t][:, lo:hi], r_tab[t][:].indirect(offsets[:, lo // 16 : hi // 16]), carry[t][:, lo:hi], ALU.mult)
 
         def blend(t, lo, hi):
@@ -184,17 +183,18 @@ def tile_list_hwayt_dl_reluP_kernel(
                 out=y[t][:, lo:hi], in0=made[t, lo // HALF][:, lo:hi], scalar=0.0, in1=parts[t][:, lo:hi], op0=ALU.min, op1=ALU.subtract, reverse1=True
             )
 
-        def blend_on_tensor(t, half):
-            turned = psum.tile([P, J - SHARE], F32, name="turned", tag="bank2")
-            for b in blocks:
-                nc.tensor.matmul(turned[:, b], made[t, 1][:, half][:, b], ident[:], start=True, stop=False, is_transpose=True)
-                nc.tensor.matmul(turned[:, b], parts[t][:, half][:, b], ident[:], start=False, stop=True, is_transpose=True)
-            staged = keep.tile([P, J - SHARE], F32, name=f"staged{t}")
+        def blend_on_tensor(t, lo, hi, bank):
+            blocks = [(slice(c, c + P), slice(c - lo, c - lo + P)) for c in range(lo, hi, P)]
+            turned = psum.tile([P, hi - lo], F32, name="turned", tag=f"bank{bank}")
+            for cols, b in blocks:
+                nc.tensor.matmul(turned[:, b], made[t, lo // HALF][:, cols], ident[:], start=True, stop=False, is_transpose=True)
+                nc.tensor.matmul(turned[:, b], parts[t][:, cols], ident[:], start=False, stop=True, is_transpose=True)
+            staged = keep.tile([P, hi - lo], F32, name=f"staged{t}_{lo}")
             nc.scalar.copy(staged[:], turned[:])
-            back = psum.tile([P, J - SHARE], F32, name="back", tag="bank3")
-            for b in blocks:
+            back = psum.tile([P, hi - lo], F32, name="back", tag=f"bank{bank + 1}")
+            for cols, b in blocks:
                 nc.tensor.transpose(back[:, b], staged[:, b], ident[:])
-            nc.scalar.copy(y[t][:, half], back[:])
+            nc.scalar.copy(y[t][:, lo:hi], back[:])
 
         for h in range(2):
             gates(0, h)
@@ -221,11 +221,12 @@ def tile_list_hwayt_dl_reluP_kernel(
                 nc.gpsimd.tensor_tensor(y[t][:, first], parts[t][:, first], made[t, 0][:, first], ALU.add)
                 if t == 1:
                     round_early(first)
-                blend_on_tensor(t, second)
+                blend_on_tensor(t, SHARE, J, 2)
                 if t == 1:
                     round_early(second)
             else:
-                blend(t, 0, HALF)
+                blend_on_tensor(t, 0, HALF // 2, 4)
+                blend_on_tensor(t, HALF // 2, HALF, 6)
                 blend(t, HALF, J)
             nc.sync.dma_start(out=y_rows[t], in_=y[t])
 
@@ -236,7 +237,7 @@ def tile_list_hwayt_dl_reluP_kernel(
         edges = [sum(TAIL[:i]) for i in range(len(TAIL) + 1)]
         spans = list(zip(edges[:-1], edges[1:]))
 
-        stored_after = {1: 0, 2: 2, 4: 3}
+        stored_after = {1: 0, 2: 2, 3: 3}
 
         def finish(i):
             lo, hi = spans[i]
@@ -255,7 +256,7 @@ def tile_list_hwayt_dl_reluP_kernel(
                 nc.sync.dma_start(out=y_rows[last][:, lo2:hi], in_=y[last][:, lo2:hi])
             if i >= 1:
                 finish(i - 1)
-            copy = nc.vector.tensor_copy if i == len(spans) - 1 else nc.scalar.copy
+            copy = nc.vector.tensor_copy if i >= len(spans) - 1 else nc.scalar.copy
             copy(out=y_bf[:, lo:hi, 2:4], in_=y_hi[:, :, lo:hi].rearrange("p t j -> p j t"))
         finish(len(spans) - 1)
         for r in range(4):

@@ -59,10 +59,10 @@ def tile_list_hwayt_dl_reluP_kernel(
         tab_w = keep.tile([P, T], U32, name="tab_w", align_bytes=64)
         tab_rows = tab_words[0].rearrange("p n i -> p (n i)").bitcast(I32)
         nc.sync.dma_start(out=tab_w[:, : T // 2].bitcast(I32), in_=tab_rows[:, : T // 2])
-        load_scale_rows(nc.sync, tab_s, tab_scales)
-        nc.sync.dma_start(out=tab_w[:, T // 2 :].bitcast(I32), in_=tab_rows[:, T // 2 :])
         bias = keep.tile([P, PACK], F32, name="bias")
         nc.sync.dma_start(out=bias[:], in_=bg.rearrange("(p t) -> p t", t=PACK))
+        load_scale_rows(nc.sync, tab_s, tab_scales)
+        nc.sync.dma_start(out=tab_w[:, T // 2 :].bitcast(I32), in_=tab_rows[:, T // 2 :])
         load_scale_rows(nc.sync, wh4_s_raw, wh4_scales)
         whd_raw = keep.tile([P, PACK, N], F32, name="whd_raw")
         nc.sync.dma_start(out=whd_raw[:], in_=whd.rearrange("(p i) n -> p i n", i=PACK))
@@ -183,17 +183,22 @@ def tile_list_hwayt_dl_reluP_kernel(
                 out=y[t][:, lo:hi], in0=made[t, lo // HALF][:, lo:hi], scalar=0.0, in1=parts[t][:, lo:hi], op0=ALU.min, op1=ALU.subtract, reverse1=True
             )
 
-        def blend_on_tensor(t, lo, hi, bank):
-            blocks = [(slice(c, c + P), slice(c - lo, c - lo + P)) for c in range(lo, hi, P)]
+        def turn(dst, src, start, stop):
+            width = dst.shape[1]
+            for c in range(0, width, P):
+                nc.tensor.matmul(dst[:, c : c + P], src[:, c : c + P], ident[:], start=start and c == 0, stop=stop and c == width - P, is_transpose=True)
+
+        def open_sum(t, lo, hi, bank):
             turned = psum.tile([P, hi - lo], F32, name="turned", tag=f"bank{bank}")
-            for cols, b in blocks:
-                nc.tensor.matmul(turned[:, b], made[t, lo // HALF][:, cols], ident[:], start=True, stop=False, is_transpose=True)
-                nc.tensor.matmul(turned[:, b], parts[t][:, cols], ident[:], start=False, stop=True, is_transpose=True)
+            turn(turned[:], made[t, lo // HALF][:, lo:hi], True, False)
+            return turned
+
+        def close_sum(t, lo, hi, turned, bank):
+            turn(turned[:], parts[t][:, lo:hi], False, True)
             staged = keep.tile([P, hi - lo], F32, name=f"staged{t}_{lo}")
             nc.scalar.copy(staged[:], turned[:])
-            back = psum.tile([P, hi - lo], F32, name="back", tag=f"bank{bank + 1}")
-            for cols, b in blocks:
-                nc.tensor.transpose(back[:, b], staged[:, b], ident[:])
+            back = psum.tile([P, hi - lo], F32, name="back", tag=f"bank{bank}")
+            turn(back[:], staged[:], True, True)
             nc.scalar.copy(y[t][:, lo:hi], back[:])
 
         for h in range(2):
@@ -212,21 +217,25 @@ def tile_list_hwayt_dl_reluP_kernel(
         def round_early(half):
             nc.scalar.copy(out=y_bf[:, half, 0:2], in_=y_lo[:, :, half].rearrange("p t j -> p j t"))
 
+        quarters = ((0, HALF // 2), (HALF // 2, HALF))
         behind_gather = (((1, 0), (1, 1), (2, 0)), ((2, 1), (3, 0), (3, 1)), ())
         for t in range(PACK - 1):
             kept(t, 0, J)
             for u, h in behind_gather[t]:
                 gated(u, h)
             if t < 2:
-                nc.gpsimd.tensor_tensor(y[t][:, first], parts[t][:, first], made[t, 0][:, first], ALU.add)
-                if t == 1:
-                    round_early(first)
-                blend_on_tensor(t, SHARE, J, 2)
+                for cols in ((first,), (slice(0, SHARE // 2), slice(SHARE // 2, SHARE)))[t]:
+                    nc.gpsimd.tensor_tensor(y[t][:, cols], parts[t][:, cols], made[t, 0][:, cols], ALU.add)
+                    if t == 1:
+                        round_early(cols)
+                close_sum(t, SHARE, J, open_sum(t, SHARE, J, 2), 3)
+                if t == 0:
+                    opened = [open_sum(2, lo, hi, 4 + i) for i, (lo, hi) in enumerate(quarters)]
                 if t == 1:
                     round_early(second)
             else:
-                blend_on_tensor(t, 0, HALF // 2, 4)
-                blend_on_tensor(t, HALF // 2, HALF, 6)
+                for i, (lo, hi) in enumerate(quarters):
+                    close_sum(t, lo, hi, opened[i], 6 + i)
                 blend(t, HALF, J)
             nc.sync.dma_start(out=y_rows[t], in_=y[t])
 

@@ -131,7 +131,7 @@ def tile_list_hwayt_dl_reluP_kernel(
                 carry[t] = keep.tile([P, J], F32, name=f"carry{t}", tag=f"carry{t}")
                 if (t, h) in on_tensor:
                     gate[t] = keep.tile([P, J], F32, name=f"gate{t}")
-            ga = psum.tile([P, HALF], F32, name="ga", tag=f"bank{2 * min(t, 1) + h}")
+            ga = psum.tile([P, HALF], F32, name="ga", tag=f"bank{((0, 1), (7, 2), (3, 2), (3, 2))[t][h]}")
             nc.tensor.matmul_mx(
                 out=ga[:], lhsT=wg_w[:, cols].bitcast(FP8X4), lhsT_scale=wg_s[:, cols],
                 rhs=got_w[h][:].bitcast(FP8X4), rhs_scale=got_s[h][:], start=True, stop=True,
@@ -144,7 +144,7 @@ def tile_list_hwayt_dl_reluP_kernel(
 
         def transform(t, h):
             cols = slice(t * P, (t + 1) * P)
-            ha = psum.tile([P, HALF], F32, name="ha", tag=f"bank{2 * ((t + 1) % PACK) + h}")
+            ha = psum.tile([P, HALF], F32, name="ha", tag=f"bank{((2, 3), (4, 5), (6, 4), (5, 6))[t][h]}")
             passes = [
                 (wh4_w[:, 2 * t * P : 2 * (t + 1) * P].bitcast(FP4X4), wh4_s[:, cols]),
                 (whd_w[:, cols].bitcast(FP8X4), whd_s[:, cols]),
@@ -228,14 +228,14 @@ def tile_list_hwayt_dl_reluP_kernel(
                     nc.gpsimd.tensor_tensor(y[t][:, cols], parts[t][:, cols], made[t, 0][:, cols], ALU.add)
                     if t == 1:
                         round_early(cols)
-                close_sum(t, SHARE, J, open_sum(t, SHARE, J, 2), 3)
+                close_sum(t, SHARE, J, open_sum(t, SHARE, J, 3), 2)
                 if t == 0:
-                    opened = [open_sum(2, lo, hi, 4 + i) for i, (lo, hi) in enumerate(quarters)]
+                    opened = [open_sum(2, lo, hi, i) for i, (lo, hi) in enumerate(quarters)]
                 if t == 1:
                     round_early(second)
             else:
                 for i, (lo, hi) in enumerate(quarters):
-                    close_sum(t, lo, hi, opened[i], 6 + i)
+                    close_sum(t, lo, hi, opened[i], (7, 4)[i])
                 blend(t, HALF, J)
             nc.sync.dma_start(out=y_rows[t], in_=y[t])
 

@@ -21,6 +21,7 @@ P = 128
 PACK = 4
 HALF = 512
 SHARE = 768
+CUTS = (1536, 3072)
 TAIL = (256, 256, 256, 256)
 
 
@@ -43,7 +44,7 @@ def tile_list_hwayt_dl_reluP_kernel(
         tab_s = keep.tile([P, T], U8, name="tab_s", align_bytes=64)
         nc.vector.memset(tab_s[:, : T // 2].bitcast(I32), 0)
         wg_s_raw = keep.tile([P, N], U8, name="wg_s_raw", align_bytes=64)
-        wh4_s_raw = keep.tile([P, N], U8, name="wh4_s_raw", tag="late", align_bytes=64)
+        wh4_s_raw = keep.tile([P, N], U8, name="wh4_s_raw", align_bytes=64)
         nc.gpsimd.memset(wg_s_raw[:].bitcast(I32), 0)
         nc.gpsimd.memset(tab_s[:, T // 2 :].bitcast(I32), 0)
         nc.gpsimd.memset(wh4_s_raw[:].bitcast(I32), 0)
@@ -58,12 +59,17 @@ def tile_list_hwayt_dl_reluP_kernel(
         load_scale_rows(nc.sync, wg_s_raw, wg_scales)
         tab_w = keep.tile([P, T], U32, name="tab_w", align_bytes=64)
         tab_rows = tab_words[0].rearrange("p n i -> p (n i)").bitcast(I32)
-        nc.sync.dma_start(out=tab_w[:, : T // 2].bitcast(I32), in_=tab_rows[:, : T // 2])
+
+        def load_words(lo, hi):
+            nc.sync.dma_start(out=tab_w[:, lo:hi].bitcast(I32), in_=tab_rows[:, lo:hi])
+
+        load_words(0, CUTS[0])
         bias = keep.tile([P, PACK], F32, name="bias")
         nc.sync.dma_start(out=bias[:], in_=bg.rearrange("(p t) -> p t", t=PACK))
         load_scale_rows(nc.sync, tab_s, tab_scales)
-        nc.sync.dma_start(out=tab_w[:, T // 2 :].bitcast(I32), in_=tab_rows[:, T // 2 :])
+        load_words(CUTS[0], CUTS[1])
         load_scale_rows(nc.sync, wh4_s_raw, wh4_scales)
+        load_words(CUTS[1], T)
         whd_raw = keep.tile([P, PACK, N], F32, name="whd_raw")
         nc.sync.dma_start(out=whd_raw[:], in_=whd.rearrange("(p i) n -> p i n", i=PACK))
         r_rows = rT.rearrange("(p t) c -> t p c", t=PACK)
@@ -101,12 +107,11 @@ def tile_list_hwayt_dl_reluP_kernel(
             s_h = keep.tile([P, HALF], U8, name=f"got_s{h}", align_bytes=64)
             nc.vector.tensor_copy(s_h[:], tab_s[:].indirect(offsets[:, h * 32 : (h + 1) * 32]))
             got_s.append(s_h)
+        deal_scales(wh4_s, wh4_s_raw)
         for h in range(2):
-            w_h = keep.tile([P, HALF], U32, name=f"got_w{h}", tag=("got_w0", "late")[h], align_bytes=64)
+            w_h = keep.tile([P, HALF], U32, name=f"got_w{h}", align_bytes=64)
             nc.vector.tensor_copy(w_h[:], tab_w[:].indirect(offsets[:, h * 32 : (h + 1) * 32]))
             got_w.append(w_h)
-            if h == 0:
-                deal_scales(wh4_s, wh4_s_raw)
         whd_w = keep.tile([P, N], U32, name="whd_w", align_bytes=64)
         whd_s = keep.tile([P, N], U8, name="whd_s", align_bytes=64)
         for u, copy in enumerate((nc.vector.tensor_copy, nc.vector.tensor_copy)):
@@ -144,7 +149,7 @@ def tile_list_hwayt_dl_reluP_kernel(
 
         def transform(t, h):
             cols = slice(t * P, (t + 1) * P)
-            ha = psum.tile([P, HALF], F32, name="ha", tag=f"bank{((2, 3), (4, 5), (6, 4), (5, 6))[t][h]}")
+            ha = psum.tile([P, HALF], F32, name="ha", tag=f"bank{2 * ((t + 1) % PACK) + h}")
             passes = [
                 (wh4_w[:, 2 * t * P : 2 * (t + 1) * P].bitcast(FP4X4), wh4_s[:, cols]),
                 (whd_w[:, cols].bitcast(FP8X4), whd_s[:, cols]),
@@ -173,14 +178,19 @@ def tile_list_hwayt_dl_reluP_kernel(
                     out=made[t, h][:, halves[h]], in0=carry[t][:, halves[h]], scalar=1.0, in1=sums[t, h][:], op0=ALU.subtract, op1=ALU.mult
                 )
 
+        def new_part(t, lo, hi, tag):
+            parts[t, lo, hi] = keep.tile([P, hi - lo], F32, name=f"kept{t}_{lo}", tag=tag)
+
+        def part(t, lo, hi):
+            start, end = [(a, b) for u, a, b in parts if u == t and a <= lo and hi <= b][0]
+            return parts[t, start, end][:, lo - start : hi - start]
+
         def kept(t, lo, hi):
-            if lo == 0:
-                parts[t] = keep.tile([P, J], F32, name=f"kept{t}", tag=("kept0", "kept1", "kept2", "carry1")[t])
-            nc.vector.tensor_tensor(parts[t][:, lo:hi], r_tab[t][:].indirect(offsets[:, lo // 16 : hi // 16]), carry[t][:, lo:hi], ALU.mult)
+            nc.vector.tensor_tensor(part(t, lo, hi), r_tab[t][:].indirect(offsets[:, lo // 16 : hi // 16]), carry[t][:, lo:hi], ALU.mult)
 
         def blend(t, lo, hi):
             nc.vector.scalar_tensor_tensor(
-                out=y[t][:, lo:hi], in0=made[t, lo // HALF][:, lo:hi], scalar=0.0, in1=parts[t][:, lo:hi], op0=ALU.min, op1=ALU.subtract, reverse1=True
+                out=y[t][:, lo:hi], in0=made[t, lo // HALF][:, lo:hi], scalar=0.0, in1=part(t, lo, hi), op0=ALU.min, op1=ALU.subtract, reverse1=True
             )
 
         def turn(dst, src, start, stop):
@@ -194,8 +204,8 @@ def tile_list_hwayt_dl_reluP_kernel(
             return turned
 
         def close_sum(t, lo, hi, turned, bank):
-            turn(turned[:], parts[t][:, lo:hi], False, True)
-            staged = keep.tile([P, hi - lo], F32, name=f"staged{t}_{lo}")
+            turn(turned[:], part(t, lo, hi), False, True)
+            staged = keep.tile([P, hi - lo], F32, name=f"staged{t}_{lo}", tag=f"staged{t}_{lo}", align_bytes=64)
             nc.scalar.copy(staged[:], turned[:])
             back = psum.tile([P, hi - lo], F32, name="back", tag=f"bank{bank}")
             turn(back[:], staged[:], True, True)
@@ -211,31 +221,42 @@ def tile_list_hwayt_dl_reluP_kernel(
                 gates(t, h)
             for h in range(2):
                 transform(t, h)
-        y_bf = keep.tile([P, J, PACK], BF16, name="y_bf", align_bytes=64)
         first, second = slice(0, SHARE), slice(SHARE, J)
+        woven = {SHARE: keep.tile([P, J - SHARE, PACK], BF16, name="y_bf_rest", align_bytes=64)}
 
-        def round_early(half):
-            nc.scalar.copy(out=y_bf[:, half, 0:2], in_=y_lo[:, :, half].rearrange("p t j -> p j t"))
+        def y_bf(lo, hi):
+            base = SHARE if lo >= SHARE else 0
+            return woven[base][:, lo - base : hi - base, :]
+
+        def round_early(cols):
+            nc.scalar.copy(out=y_bf(cols.start, cols.stop)[:, :, 0:2], in_=y_lo[:, :, cols].rearrange("p t j -> p j t"))
 
         quarters = ((0, HALF // 2), (HALF // 2, HALF))
         behind_gather = (((1, 0), (1, 1), (2, 0)), ((2, 1), (3, 0), (3, 1)), ())
+        gathers = (((0, J),), ((SHARE, J), (0, SHARE)), ((0, HALF), (HALF, J)))
         for t in range(PACK - 1):
-            kept(t, 0, J)
+            for lo, hi in gathers[t]:
+                new_part(t, lo, hi, f"kept{t}_{lo}")
+                kept(t, lo, hi)
+            if t == 1:
+                close_sum(t, SHARE, J, rest, 4)
+                round_early(second)
+                woven[0] = keep.tile([P, SHARE, PACK], BF16, name="y_bf", tag=f"staged1_{SHARE}", align_bytes=64)
+            if t == 2:
+                for i, (lo, hi) in enumerate(quarters):
+                    close_sum(t, lo, hi, opened[i], 2 + i)
             for u, h in behind_gather[t]:
                 gated(u, h)
-            if t < 2:
-                for cols in ((first,), (slice(0, SHARE // 2), slice(SHARE // 2, SHARE)))[t]:
-                    nc.gpsimd.tensor_tensor(y[t][:, cols], parts[t][:, cols], made[t, 0][:, cols], ALU.add)
-                    if t == 1:
-                        round_early(cols)
+            if t == 0:
+                nc.gpsimd.tensor_tensor(y[t][:, first], part(t, 0, SHARE), made[t, 0][:, first], ALU.add)
                 close_sum(t, SHARE, J, open_sum(t, SHARE, J, 3), 2)
-                if t == 0:
-                    opened = [open_sum(2, lo, hi, i) for i, (lo, hi) in enumerate(quarters)]
-                if t == 1:
-                    round_early(second)
-            else:
-                for i, (lo, hi) in enumerate(quarters):
-                    close_sum(t, lo, hi, opened[i], (7, 4)[i])
+                rest = open_sum(1, SHARE, J, 4)
+                opened = [open_sum(2, lo, hi, 5 + i) for i, (lo, hi) in enumerate(quarters)]
+            if t == 1:
+                for cols in (slice(0, SHARE // 2), slice(SHARE // 2, SHARE)):
+                    nc.gpsimd.tensor_tensor(y[t][:, cols], part(t, cols.start, cols.stop), made[t, 0][:, cols], ALU.add)
+                    round_early(cols)
+            if t == 2:
                 blend(t, HALF, J)
             nc.sync.dma_start(out=y_rows[t], in_=y[t])
 
@@ -250,11 +271,12 @@ def tile_list_hwayt_dl_reluP_kernel(
 
         def finish(i):
             lo, hi = spans[i]
-            nc.vector.quantize_mx(out=y_w[:, lo:hi].bitcast(FP8X4), scales=y_s[:, lo:hi], in_=y_bf[:, lo:hi, :].rearrange("p j t -> p (j t)"))
+            nc.vector.quantize_mx(out=y_w[:, lo:hi].bitcast(FP8X4), scales=y_s[:, lo:hi], in_=y_bf(lo, hi).rearrange("p j t -> p (j t)"))
             if i in stored_after:
                 lo2 = spans[stored_after[i]][0]
                 nc.sync.dma_start(out=words_out[:, lo2:hi], in_=y_w[:, lo2:hi].bitcast(I32))
 
+        new_part(last, 0, J, "carry1")
         kept(last, *spans[0])
         for i, (lo, hi) in enumerate(spans):
             if i + 1 < len(spans):
@@ -266,7 +288,7 @@ def tile_list_hwayt_dl_reluP_kernel(
             if i >= 1:
                 finish(i - 1)
             copy = nc.vector.tensor_copy if i >= len(spans) - 1 else nc.scalar.copy
-            copy(out=y_bf[:, lo:hi, 2:4], in_=y_hi[:, :, lo:hi].rearrange("p t j -> p j t"))
+            copy(out=y_bf(lo, hi)[:, :, 2:4], in_=y_hi[:, :, lo:hi].rearrange("p t j -> p j t"))
         finish(len(spans) - 1)
         for r in range(4):
             (nc.sync, nc.scalar)[r % 2].dma_start(out=out_2[0, r:16:4, :].bitcast(I32), in_=y_s[r:P:32, :].bitcast(I32))

@@ -22,7 +22,7 @@ PACK = 4
 HALF = 512
 SHARE = 768
 CUTS = (1536, 3072)
-TAIL = (256, 256, 256, 256)
+PIECE = 256
 
 
 def load_scale_rows(queue, plane, rows):
@@ -264,17 +264,14 @@ def tile_list_hwayt_dl_reluP_kernel(
         y_s = keep.tile([P, J], U8, name="y_s", align_bytes=64)
         words_out = out_1[0].rearrange("p j i -> p (j i)").bitcast(I32)
         last = PACK - 1
-        edges = [sum(TAIL[:i]) for i in range(len(TAIL) + 1)]
-        spans = list(zip(edges[:-1], edges[1:]))
+        spans = [(lo, lo + PIECE) for lo in range(0, J, PIECE)]
 
-        stored_after = {1: 0, 2: 2, 3: 3}
+        def round_late(copy, lo, hi):
+            copy(out=y_bf(lo, hi)[:, :, 2:4], in_=y_hi[:, :, lo:hi].rearrange("p t j -> p j t"))
 
-        def finish(i):
-            lo, hi = spans[i]
+        def finish(lo, hi):
             nc.vector.quantize_mx(out=y_w[:, lo:hi].bitcast(FP8X4), scales=y_s[:, lo:hi], in_=y_bf(lo, hi).rearrange("p j t -> p (j t)"))
-            if i in stored_after:
-                lo2 = spans[stored_after[i]][0]
-                nc.sync.dma_start(out=words_out[:, lo2:hi], in_=y_w[:, lo2:hi].bitcast(I32))
+            nc.sync.dma_start(out=words_out[:, lo:hi], in_=y_w[:, lo:hi].bitcast(I32))
 
         new_part(last, 0, J, "carry1")
         kept(last, *spans[0])
@@ -282,13 +279,13 @@ def tile_list_hwayt_dl_reluP_kernel(
             if i + 1 < len(spans):
                 kept(last, *spans[i + 1])
             blend(last, lo, hi)
-            if i in stored_after:
-                lo2 = spans[stored_after[i]][0]
-                nc.sync.dma_start(out=y_rows[last][:, lo2:hi], in_=y[last][:, lo2:hi])
-            if i >= 1:
-                finish(i - 1)
-            copy = nc.vector.tensor_copy if i >= len(spans) - 1 else nc.scalar.copy
-            copy(out=y_bf(lo, hi)[:, :, 2:4], in_=y_hi[:, :, lo:hi].rearrange("p t j -> p j t"))
-        finish(len(spans) - 1)
+            if i != len(spans) - 2:
+                round_late(nc.scalar.copy, lo, hi)
+            if i % 2 == 1:
+                nc.sync.dma_start(out=y_rows[last][:, halves[i // 2]], in_=y[last][:, halves[i // 2]])
+        round_late(nc.vector.tensor_copy, *spans[-2])
+        finish(0, HALF)
+        for lo, hi in spans[2:]:
+            finish(lo, hi)
         for r in range(4):
             (nc.sync, nc.scalar)[r % 2].dma_start(out=out_2[0, r:16:4, :].bitcast(I32), in_=y_s[r:P:32, :].bitcast(I32))

@@ -21,13 +21,7 @@ P = 128
 PACK = 4
 HALF = 512
 SHARE = 768
-CUTS = (1536, 3072)
 PIECE = 256
-
-
-def load_scale_rows(queue, plane, rows):
-    for r in range(4):
-        queue.dma_start(out=plane[r:P:32, :].bitcast(I32), in_=rows[0, r:16:4, :].bitcast(I32))
 
 
 def tile_list_hwayt_dl_reluP_kernel(
@@ -38,90 +32,82 @@ def tile_list_hwayt_dl_reluP_kernel(
         keep = ctx.enter_context(tc.tile_pool(name="keep", bufs=1))
         psum = ctx.enter_context(tc.psum_pool(name="psum", bufs=1))
 
+        def tile(shape, dtype, name, tag=None):
+            return keep.tile(shape, dtype, name=name, tag=tag or name, align_bytes=64)
+
         offsets = keep.tile([P, J // 16], U16, name="offsets")
         nc.sync.dma_start(offsets[:], offs)
 
-        tab_s = keep.tile([P, T], U8, name="tab_s", align_bytes=64)
-        nc.vector.memset(tab_s[:, : T // 2].bitcast(I32), 0)
-        wg_s_raw = keep.tile([P, N], U8, name="wg_s_raw", align_bytes=64)
-        wh4_s_raw = keep.tile([P, N], U8, name="wh4_s_raw", align_bytes=64)
-        nc.gpsimd.memset(wg_s_raw[:].bitcast(I32), 0)
+        tab_s = tile([P, T], U8, "tab_s")
+        w_s_raw = tile([P, 2 * N], U8, "w_s_raw")
+        nc.gpsimd.memset(w_s_raw[:].bitcast(I32), 0)
         nc.gpsimd.memset(tab_s[:, T // 2 :].bitcast(I32), 0)
-        nc.gpsimd.memset(wh4_s_raw[:].bitcast(I32), 0)
+        nc.vector.memset(tab_s[:, : T // 2].bitcast(I32), 0)
 
-        ident = keep.tile([P, P], F32, name="ident")
+        ident = tile([P, P], F32, "ident")
         make_identity(nc, ident[:])
 
-        wg_raw = keep.tile([P, N], U32, name="wg_raw", align_bytes=64)
+        wg_raw = tile([P, N], U32, "wg_raw")
         nc.sync.dma_start(out=wg_raw[:].bitcast(I32), in_=wg_words[0].rearrange("p n i -> p (n i)").bitcast(I32))
-        wh4_raw = keep.tile([P, 2 * N], U8, name="wh4_raw", align_bytes=64)
+        wh4_raw = tile([P, N], U16, "wh4_raw")
         nc.sync.dma_start(out=wh4_raw[:].bitcast(I32), in_=wh4_words[0].bitcast(I32))
-        load_scale_rows(nc.sync, wg_s_raw, wg_scales)
-        tab_w = keep.tile([P, T], U32, name="tab_w", align_bytes=64)
-        tab_rows = tab_words[0].rearrange("p n i -> p (n i)").bitcast(I32)
-
-        def load_words(lo, hi):
-            nc.sync.dma_start(out=tab_w[:, lo:hi].bitcast(I32), in_=tab_rows[:, lo:hi])
-
-        load_words(0, CUTS[0])
-        bias = keep.tile([P, PACK], F32, name="bias")
+        bias = tile([P, PACK], F32, "bias")
         nc.sync.dma_start(out=bias[:], in_=bg.rearrange("(p t) -> p t", t=PACK))
-        load_scale_rows(nc.sync, tab_s, tab_scales)
-        load_words(CUTS[0], CUTS[1])
-        load_scale_rows(nc.sync, wh4_s_raw, wh4_scales)
-        load_words(CUTS[1], T)
-        whd_raw = keep.tile([P, PACK, N], F32, name="whd_raw")
+        for w, rows in enumerate((wg_scales, wh4_scales)):
+            nc.sync.dma_start(out=w_s_raw[0:P:8, w * N : (w + 1) * N].bitcast(I32), in_=rows[0].bitcast(I32))
+        nc.sync.dma_start(out=tab_s[0:P:8, :].bitcast(I32), in_=tab_scales[0].bitcast(I32))
+        tab_w = tile([P, T], U32, "tab_w")
+        nc.sync.dma_start(out=tab_w[:].bitcast(I32), in_=tab_words[0].rearrange("p n i -> p (n i)").bitcast(I32))
+        whd_raw = tile([P, PACK, N], F32, "whd_raw")
         nc.sync.dma_start(out=whd_raw[:], in_=whd.rearrange("(p i) n -> p i n", i=PACK))
-        r_rows = rT.rearrange("(p t) c -> t p c", t=PACK)
-        r_tab = []
-        for t in range(PACK):
-            r_t = keep.tile([P, T], F32, name=f"r_tab{t}", tag=f"r_tab{t}")
-            nc.sync.dma_start(out=r_t[:], in_=r_rows[t])
-            r_tab.append(r_t)
 
-        neg_bias = keep.tile([P, PACK], F32, name="neg_bias")
+        neg_bias = tile([P, PACK], F32, "neg_bias")
         nc.vector.tensor_scalar(neg_bias[:], bias[:], -1.0, None, ALU.mult)
-
-        wg_w = keep.tile([P, N], U32, name="wg_w", align_bytes=64)
+        wg_w = tile([P, N], U32, "wg_w")
         nc.vector.tensor_copy(
             out=wg_w[:].bitcast(I32).rearrange("p (t m) -> p m t", t=PACK),
             in_=wg_raw[:].bitcast(I32).rearrange("p (m t) -> p m t", t=PACK),
         )
-        wh4_w = keep.tile([P, 2 * N], U8, name="wh4_w", align_bytes=64)
+        planes = tile([P, J + 2 * N], U8, "planes")
         nc.vector.tensor_copy(
-            out=wh4_w[:].rearrange("p (t m b) -> p m t b", t=PACK, b=2),
-            in_=wh4_raw[:].rearrange("p (m t b) -> p m t b", t=PACK, b=2),
+            out=planes[:, J:].rearrange("p (w t m) -> p w t m", w=2, t=PACK),
+            in_=w_s_raw[:].rearrange("p (w m t) -> p w t m", w=2, t=PACK),
         )
-        wg_s = keep.tile([P, N], U8, name="wg_s", align_bytes=64)
-        wh4_s = keep.tile([P, N], U8, name="wh4_s", align_bytes=64)
+        got_s = tile([P, J], U8, "got_s")
+        nc.vector.tensor_copy(got_s[:], tab_s[:].indirect(offsets[:]))
+        nc.vector.tensor_copy(planes[:, :J].bitcast(I32), got_s[:].bitcast(I32))
+        for r in range(1, 4):
+            nc.scalar.dma_start(out=planes[r:P:32, :].bitcast(I32), in_=planes[8 * r : P : 32, :].bitcast(I32))
+        wh4_w = tile([P, N], U16, "wh4_w", "got_s")
+        nc.vector.tensor_copy(
+            out=wh4_w[:].rearrange("p (t m) -> p m t", t=PACK), in_=wh4_raw[:].rearrange("p (m t) -> p m t", t=PACK)
+        )
+        wg_s, wh4_s = planes[:, J : J + N], planes[:, J + N :]
 
-        def deal_scales(dst, src):
-            nc.vector.tensor_copy(
-                out=dst[:].rearrange("p (t m) -> p m t", t=PACK), in_=src[:].rearrange("p (m t) -> p m t", t=PACK)
-            )
-
-        deal_scales(wg_s, wg_s_raw)
         halves = [slice(h * HALF, (h + 1) * HALF) for h in range(J // HALF)]
-        got_s, got_w = [], []
+        got_w = []
         for h in range(2):
-            s_h = keep.tile([P, HALF], U8, name=f"got_s{h}", align_bytes=64)
-            nc.vector.tensor_copy(s_h[:], tab_s[:].indirect(offsets[:, h * 32 : (h + 1) * 32]))
-            got_s.append(s_h)
-        deal_scales(wh4_s, wh4_s_raw)
-        for h in range(2):
-            w_h = keep.tile([P, HALF], U32, name=f"got_w{h}", align_bytes=64)
+            w_h = tile([P, HALF], U32, f"got_w{h}")
             nc.vector.tensor_copy(w_h[:], tab_w[:].indirect(offsets[:, h * 32 : (h + 1) * 32]))
             got_w.append(w_h)
-        whd_w = keep.tile([P, N], U32, name="whd_w", align_bytes=64)
-        whd_s = keep.tile([P, N], U8, name="whd_s", align_bytes=64)
-        for u, copy in enumerate((nc.vector.tensor_copy, nc.vector.tensor_copy)):
-            whd_bf = keep.tile([P, PACK * N // 2], BF16, name=f"whd_bf{u}", align_bytes=64)
-            copy(
+        whd_w = tile([P, N], U32, "whd_w")
+        whd_s = tile([P, N], U8, "whd_s")
+        for u in range(2):
+            whd_bf = tile([P, PACK * N // 2], BF16, f"whd_bf{u}")
+            nc.vector.tensor_copy(
                 out=whd_bf[:].rearrange("p (t m i) -> p m t i", t=2, i=PACK),
                 in_=whd_raw[:].rearrange("p i (m t) -> p m t i", t=PACK)[:, :, 2 * u : 2 * u + 2, :],
             )
             cols = slice(u * N // 2, (u + 1) * N // 2)
             nc.vector.quantize_mx(out=whd_w[:, cols].bitcast(FP8X4), scales=whd_s[:, cols], in_=whd_bf[:])
+
+        r_rows = rT.rearrange("(p t) c -> t p c", t=PACK)
+        r_tags = ("wh4_raw", "tab_w", "whd_raw", "whd_bf0")
+        r_tab = []
+        for t in range(PACK):
+            r_t = tile([P, T], F32, f"r_tab{t}", r_tags[t])
+            nc.sync.dma_start(out=r_t[:], in_=r_rows[t])
+            r_tab.append(r_t)
 
         y_lo = keep.tile([P, 2, J], F32, name="y_lo")
         y_hi = keep.tile([P, 2, J], F32, name="y_hi")
@@ -133,13 +119,13 @@ def tile_list_hwayt_dl_reluP_kernel(
         def gates(t, h):
             cols = slice(t * P, (t + 1) * P)
             if h == 0:
-                carry[t] = keep.tile([P, J], F32, name=f"carry{t}", tag=f"carry{t}")
+                carry[t] = tile([P, J], F32, f"carry{t}")
                 if (t, h) in on_tensor:
                     gate[t] = keep.tile([P, J], F32, name=f"gate{t}")
             ga = psum.tile([P, HALF], F32, name="ga", tag=f"bank{((0, 1), (7, 2), (3, 2), (3, 2))[t][h]}")
             nc.tensor.matmul_mx(
                 out=ga[:], lhsT=wg_w[:, cols].bitcast(FP8X4), lhsT_scale=wg_s[:, cols],
-                rhs=got_w[h][:].bitcast(FP8X4), rhs_scale=got_s[h][:], start=True, stop=True,
+                rhs=got_w[h][:].bitcast(FP8X4), rhs_scale=planes[:, halves[h]], start=True, stop=True,
             )
             reads = [(carry[t], neg_bias, -1.0)]
             if (t, h) in on_tensor:
@@ -151,7 +137,7 @@ def tile_list_hwayt_dl_reluP_kernel(
             cols = slice(t * P, (t + 1) * P)
             ha = psum.tile([P, HALF], F32, name="ha", tag=f"bank{2 * ((t + 1) % PACK) + h}")
             passes = [
-                (wh4_w[:, 2 * t * P : 2 * (t + 1) * P].bitcast(FP4X4), wh4_s[:, cols]),
+                (wh4_w[:, cols].bitcast(U8).bitcast(FP4X4), wh4_s[:, cols]),
                 (whd_w[:, cols].bitcast(FP8X4), whd_s[:, cols]),
             ]
             if t > 0:
@@ -159,14 +145,14 @@ def tile_list_hwayt_dl_reluP_kernel(
             for i, (codes, scales) in enumerate(passes):
                 nc.tensor.matmul_mx(
                     out=ha[:], lhsT=codes, lhsT_scale=scales,
-                    rhs=got_w[h][:].bitcast(FP8X4), rhs_scale=got_s[h][:], start=i == 0, stop=i == 1,
+                    rhs=got_w[h][:].bitcast(FP8X4), rhs_scale=planes[:, halves[h]], start=i == 0, stop=i == 1,
                 )
             sums[t, h] = ha
 
         def gated(t, h):
-            behind = {(0, 0): "made00", (1, 0): "carry0", (2, 0): "r_tab0", (2, 1): "carry1", (3, 0): "r_tab1"}
+            behind = {(0, 0): "made00", (1, 0): "carry0", (2, 0): r_tags[0], (2, 1): "carry1", (3, 0): r_tags[1]}
             if (t, h) in behind:
-                made[t, h] = keep.tile([P, J], F32, name=f"made{t}_{h}", tag=behind[t, h])
+                made[t, h] = tile([P, J], F32, f"made{t}_{h}", behind[t, h])
             else:
                 made[t, h] = made[t, 0]
             if (t, h) in on_tensor:
@@ -179,7 +165,7 @@ def tile_list_hwayt_dl_reluP_kernel(
                 )
 
         def new_part(t, lo, hi, tag):
-            parts[t, lo, hi] = keep.tile([P, hi - lo], F32, name=f"kept{t}_{lo}", tag=tag)
+            parts[t, lo, hi] = tile([P, hi - lo], F32, f"kept{t}_{lo}", tag)
 
         def part(t, lo, hi):
             start, end = [(a, b) for u, a, b in parts if u == t and a <= lo and hi <= b][0]

@@ -58,16 +58,16 @@ def tile_list_hwayt_dl_reluP_kernel(
         nc.sync.dma_start(out=tab_s[0:P:8, :].bitcast(I32), in_=tab_scales[0].bitcast(I32))
         tab_w = tile([P, T], U32, "tab_w")
         nc.sync.dma_start(out=tab_w[:].bitcast(I32), in_=tab_words[0].rearrange("p n i -> p (n i)").bitcast(I32))
-        whd_raw = tile([P, PACK, N], F32, "whd_raw")
-        nc.sync.dma_start(out=whd_raw[:], in_=whd.rearrange("(p i) n -> p i n", i=PACK))
+        whd_rows = whd.rearrange("(p i) n -> p i n", i=PACK)
+        whd_raw = [tile([P, PACK, N // 2], F32, "whd_raw0")]
+        nc.sync.dma_start(out=whd_raw[0][:], in_=whd_rows[:, :, : N // 2])
 
         neg_bias = tile([P, PACK], F32, "neg_bias")
         nc.vector.tensor_scalar(neg_bias[:], bias[:], -1.0, None, ALU.mult)
         wg_w = tile([P, N], U32, "wg_w")
-        nc.vector.tensor_copy(
-            out=wg_w[:].bitcast(I32).rearrange("p (t m) -> p m t", t=PACK),
-            in_=wg_raw[:].bitcast(I32).rearrange("p (m t) -> p m t", t=PACK),
-        )
+        wh4_w = tile([P, N], U16, "wh4_w")
+        for dealt, raw in ((wg_w, wg_raw), (wh4_w, wh4_raw)):
+            nc.scalar.copy(out=dealt[:].rearrange("p (t m) -> p m t", t=PACK), in_=raw[:].rearrange("p (m t) -> p m t", t=PACK))
         planes = tile([P, J + 2 * N], U8, "planes")
         nc.vector.tensor_copy(
             out=planes[:, J:].rearrange("p (w t m) -> p w t m", w=2, t=PACK),
@@ -77,11 +77,9 @@ def tile_list_hwayt_dl_reluP_kernel(
         nc.vector.tensor_copy(got_s[:], tab_s[:].indirect(offsets[:]))
         nc.vector.tensor_copy(planes[:, :J].bitcast(I32), got_s[:].bitcast(I32))
         for r in range(1, 4):
-            nc.scalar.dma_start(out=planes[r:P:32, :].bitcast(I32), in_=planes[8 * r : P : 32, :].bitcast(I32))
-        wh4_w = tile([P, N], U16, "wh4_w", "got_s")
-        nc.vector.tensor_copy(
-            out=wh4_w[:].rearrange("p (t m) -> p m t", t=PACK), in_=wh4_raw[:].rearrange("p (m t) -> p m t", t=PACK)
-        )
+            nc.sync.dma_start(out=planes[r:P:32, :].bitcast(I32), in_=planes[8 * r : P : 32, :].bitcast(I32))
+        whd_raw.append(tile([P, PACK, N // 2], F32, "whd_raw1", "got_s"))
+        nc.sync.dma_start(out=whd_raw[1][:], in_=whd_rows[:, :, N // 2 :])
         wg_s, wh4_s = planes[:, J : J + N], planes[:, J + N :]
 
         halves = [slice(h * HALF, (h + 1) * HALF) for h in range(J // HALF)]
@@ -92,17 +90,21 @@ def tile_list_hwayt_dl_reluP_kernel(
             got_w.append(w_h)
         whd_w = tile([P, N], U32, "whd_w")
         whd_s = tile([P, N], U8, "whd_s")
+        whd_bf = tile([P, PACK, P, PACK], BF16, "whd_bf")
         for u in range(2):
-            whd_bf = tile([P, PACK * N // 2], BF16, f"whd_bf{u}")
             nc.vector.tensor_copy(
-                out=whd_bf[:].rearrange("p (t m i) -> p m t i", t=2, i=PACK),
-                in_=whd_raw[:].rearrange("p i (m t) -> p m t i", t=PACK)[:, :, 2 * u : 2 * u + 2, :],
+                out=whd_bf[:, :, u * P // 2 : (u + 1) * P // 2, :].rearrange("p t m i -> p m t i"),
+                in_=whd_raw[u][:].rearrange("p i (m t) -> p m t i", t=PACK),
             )
+        for u in range(2):
             cols = slice(u * N // 2, (u + 1) * N // 2)
-            nc.vector.quantize_mx(out=whd_w[:, cols].bitcast(FP8X4), scales=whd_s[:, cols], in_=whd_bf[:])
+            nc.vector.quantize_mx(
+                out=whd_w[:, cols].bitcast(FP8X4), scales=whd_s[:, cols],
+                in_=whd_bf[:, 2 * u : 2 * u + 2, :, :].rearrange("p t m i -> p (t m i)"),
+            )
 
         r_rows = rT.rearrange("(p t) c -> t p c", t=PACK)
-        r_tags = ("wh4_raw", "tab_w", "whd_raw", "whd_bf0")
+        r_tags = ("tab_s", "tab_w", "whd_raw0", "whd_bf")
         r_tab = []
         for t in range(PACK):
             r_t = tile([P, T], F32, f"r_tab{t}", r_tags[t])

@@ -22,6 +22,7 @@ PACK = 4
 HALF = 512
 SHARE = 768
 PIECE = 256
+CUT = 768
 
 
 def tile_list_hwayt_dl_reluP_kernel(
@@ -41,23 +42,21 @@ def tile_list_hwayt_dl_reluP_kernel(
         tab_s = tile([P, T], U8, "tab_s")
         w_s_raw = tile([P, 2 * N], U8, "w_s_raw")
         nc.gpsimd.memset(w_s_raw[:].bitcast(I32), 0)
-        nc.gpsimd.memset(tab_s[:, T // 2 :].bitcast(I32), 0)
-        nc.vector.memset(tab_s[:, : T // 2].bitcast(I32), 0)
-
-        ident = tile([P, P], F32, "ident")
-        make_identity(nc, ident[:])
+        nc.vector.memset(tab_s[:].bitcast(I32), 0)
 
         wg_raw = tile([P, N], U32, "wg_raw")
         nc.sync.dma_start(out=wg_raw[:].bitcast(I32), in_=wg_words[0].rearrange("p n i -> p (n i)").bitcast(I32))
         wh4_raw = tile([P, N], U16, "wh4_raw")
         nc.sync.dma_start(out=wh4_raw[:].bitcast(I32), in_=wh4_words[0].bitcast(I32))
-        bias = tile([P, PACK], F32, "bias")
-        nc.sync.dma_start(out=bias[:], in_=bg.rearrange("(p t) -> p t", t=PACK))
         for w, rows in enumerate((wg_scales, wh4_scales)):
             nc.sync.dma_start(out=w_s_raw[0:P:8, w * N : (w + 1) * N].bitcast(I32), in_=rows[0].bitcast(I32))
-        nc.sync.dma_start(out=tab_s[0:P:8, :].bitcast(I32), in_=tab_scales[0].bitcast(I32))
         tab_w = tile([P, T], U32, "tab_w")
-        nc.sync.dma_start(out=tab_w[:].bitcast(I32), in_=tab_words[0].rearrange("p n i -> p (n i)").bitcast(I32))
+        tab_rows = tab_words[0].rearrange("p n i -> p (n i)").bitcast(I32)
+        nc.sync.dma_start(out=tab_w[:, :CUT].bitcast(I32), in_=tab_rows[:, :CUT])
+        nc.sync.dma_start(out=tab_s[0:P:8, :].bitcast(I32), in_=tab_scales[0].bitcast(I32))
+        nc.sync.dma_start(out=tab_w[:, CUT:].bitcast(I32), in_=tab_rows[:, CUT:])
+        bias = tile([P, PACK], F32, "bias")
+        nc.sync.dma_start(out=bias[:], in_=bg.rearrange("(p t) -> p t", t=PACK))
         whd_rows = whd.rearrange("(p i) n -> p i n", i=PACK)
         whd_raw = [tile([P, PACK, N // 2], F32, "whd_raw0")]
         nc.sync.dma_start(out=whd_raw[0][:], in_=whd_rows[:, :, : N // 2])
@@ -102,6 +101,9 @@ def tile_list_hwayt_dl_reluP_kernel(
                 out=whd_w[:, cols].bitcast(FP8X4), scales=whd_s[:, cols],
                 in_=whd_bf[:, 2 * u : 2 * u + 2, :, :].rearrange("p t m i -> p (t m i)"),
             )
+
+        ident = tile([P, P], F32, "ident", "got_s")
+        make_identity(nc, ident[:])
 
         r_rows = rT.rearrange("(p t) c -> t p c", t=PACK)
         r_tags = ("tab_s", "tab_w", "whd_raw0", "whd_bf")

@@ -57,16 +57,16 @@ def tile_list_hwayt_dl_reluP_kernel(
         nc.sync.dma_start(out=tab_w[:, CUT:].bitcast(I32), in_=tab_rows[:, CUT:])
         bias = tile([P, PACK], F32, "bias")
         nc.sync.dma_start(out=bias[:], in_=bg.rearrange("(p t) -> p t", t=PACK))
-        whd_rows = whd.rearrange("(p i) n -> p i n", i=PACK)
-        whd_raw = [tile([P, PACK, N // 2], F32, "whd_raw0")]
-        nc.sync.dma_start(out=whd_raw[0][:], in_=whd_rows[:, :, : N // 2])
+        whd_raw = tile([P, PACK, N], F32, "whd_raw")
+        nc.sync.dma_start(out=whd_raw[:], in_=whd.rearrange("(p i) n -> p i n", i=PACK))
 
         neg_bias = tile([P, PACK], F32, "neg_bias")
         nc.vector.tensor_scalar(neg_bias[:], bias[:], -1.0, None, ALU.mult)
         wg_w = tile([P, N], U32, "wg_w")
-        wh4_w = tile([P, N], U16, "wh4_w")
-        for dealt, raw in ((wg_w, wg_raw), (wh4_w, wh4_raw)):
-            nc.scalar.copy(out=dealt[:].rearrange("p (t m) -> p m t", t=PACK), in_=raw[:].rearrange("p (m t) -> p m t", t=PACK))
+        nc.scalar.copy(out=wg_w[:].rearrange("p (t m) -> p m t", t=PACK), in_=wg_raw[:].rearrange("p (m t) -> p m t", t=PACK))
+        wh4_sets = wh4_raw[:].rearrange("p (m t) -> p m t", t=PACK)
+        wh4_w = tile([P, N - P], U16, "wh4_w")
+        nc.scalar.copy(out=wh4_w[:].rearrange("p (t m) -> p m t", t=PACK - 1), in_=wh4_sets[:, :, : PACK - 1])
         planes = tile([P, J + 2 * N], U8, "planes")
         nc.vector.tensor_copy(
             out=planes[:, J:].rearrange("p (w t m) -> p w t m", w=2, t=PACK),
@@ -76,9 +76,10 @@ def tile_list_hwayt_dl_reluP_kernel(
         nc.vector.tensor_copy(got_s[:], tab_s[:].indirect(offsets[:]))
         nc.vector.tensor_copy(planes[:, :J].bitcast(I32), got_s[:].bitcast(I32))
         for r in range(1, 4):
-            nc.sync.dma_start(out=planes[r:P:32, :].bitcast(I32), in_=planes[8 * r : P : 32, :].bitcast(I32))
-        whd_raw.append(tile([P, PACK, N // 2], F32, "whd_raw1", "got_s"))
-        nc.sync.dma_start(out=whd_raw[1][:], in_=whd_rows[:, :, N // 2 :])
+            nc.scalar.dma_start(out=planes[r:P:32, :].bitcast(I32), in_=planes[8 * r : P : 32, :].bitcast(I32))
+        wh4_last = tile([P, P], U16, "wh4_last", "got_s")
+        nc.scalar.copy(out=wh4_last[:], in_=wh4_sets[:, :, PACK - 1])
+        wh4_codes = [wh4_w[:, t * P : (t + 1) * P] for t in range(PACK - 1)] + [wh4_last[:]]
         wg_s, wh4_s = planes[:, J : J + N], planes[:, J + N :]
 
         halves = [slice(h * HALF, (h + 1) * HALF) for h in range(J // HALF)]
@@ -89,24 +90,20 @@ def tile_list_hwayt_dl_reluP_kernel(
             got_w.append(w_h)
         whd_w = tile([P, N], U32, "whd_w")
         whd_s = tile([P, N], U8, "whd_s")
-        whd_bf = tile([P, PACK, P, PACK], BF16, "whd_bf")
         for u in range(2):
+            whd_bf = tile([P, PACK * N // 2], BF16, f"whd_bf{u}")
             nc.vector.tensor_copy(
-                out=whd_bf[:, :, u * P // 2 : (u + 1) * P // 2, :].rearrange("p t m i -> p m t i"),
-                in_=whd_raw[u][:].rearrange("p i (m t) -> p m t i", t=PACK),
+                out=whd_bf[:].rearrange("p (t m i) -> p m t i", t=2, i=PACK),
+                in_=whd_raw[:].rearrange("p i (m t) -> p m t i", t=PACK)[:, :, 2 * u : 2 * u + 2, :],
             )
-        for u in range(2):
             cols = slice(u * N // 2, (u + 1) * N // 2)
-            nc.vector.quantize_mx(
-                out=whd_w[:, cols].bitcast(FP8X4), scales=whd_s[:, cols],
-                in_=whd_bf[:, 2 * u : 2 * u + 2, :, :].rearrange("p t m i -> p (t m i)"),
-            )
+            nc.vector.quantize_mx(out=whd_w[:, cols].bitcast(FP8X4), scales=whd_s[:, cols], in_=whd_bf[:])
 
-        ident = tile([P, P], F32, "ident", "got_s")
+        ident = tile([P, P], F32, "ident", "whd_bf1")
         make_identity(nc, ident[:])
 
         r_rows = rT.rearrange("(p t) c -> t p c", t=PACK)
-        r_tags = ("tab_s", "tab_w", "whd_raw0", "whd_bf")
+        r_tags = ("wh4_raw", "tab_w", "whd_raw", "whd_bf0")
         r_tab = []
         for t in range(PACK):
             r_t = tile([P, T], F32, f"r_tab{t}", r_tags[t])
@@ -141,7 +138,7 @@ def tile_list_hwayt_dl_reluP_kernel(
             cols = slice(t * P, (t + 1) * P)
             ha = psum.tile([P, HALF], F32, name="ha", tag=f"bank{2 * ((t + 1) % PACK) + h}")
             passes = [
-                (wh4_w[:, cols].bitcast(U8).bitcast(FP4X4), wh4_s[:, cols]),
+                (wh4_codes[t].bitcast(U8).bitcast(FP4X4), wh4_s[:, cols]),
                 (whd_w[:, cols].bitcast(FP8X4), whd_s[:, cols]),
             ]
             if t > 0:

@@ -63,10 +63,9 @@ def tile_list_hwayt_dl_reluP_kernel(
         neg_bias = tile([P, PACK], F32, "neg_bias")
         nc.vector.tensor_scalar(neg_bias[:], bias[:], -1.0, None, ALU.mult)
         wg_w = tile([P, N], U32, "wg_w")
-        nc.scalar.copy(out=wg_w[:].rearrange("p (t m) -> p m t", t=PACK), in_=wg_raw[:].rearrange("p (m t) -> p m t", t=PACK))
-        wh4_sets = wh4_raw[:].rearrange("p (m t) -> p m t", t=PACK)
-        wh4_w = tile([P, N - P], U16, "wh4_w")
-        nc.scalar.copy(out=wh4_w[:].rearrange("p (t m) -> p m t", t=PACK - 1), in_=wh4_sets[:, :, : PACK - 1])
+        wh4_w = tile([P, N], U16, "wh4_w")
+        for dealt, raw in ((wg_w, wg_raw), (wh4_w, wh4_raw)):
+            nc.scalar.copy(out=dealt[:].rearrange("p (t m) -> p m t", t=PACK), in_=raw[:].rearrange("p (m t) -> p m t", t=PACK))
         planes = tile([P, J + 2 * N], U8, "planes")
         nc.vector.tensor_copy(
             out=planes[:, J:].rearrange("p (w t m) -> p w t m", w=2, t=PACK),
@@ -76,10 +75,7 @@ def tile_list_hwayt_dl_reluP_kernel(
         nc.vector.tensor_copy(got_s[:], tab_s[:].indirect(offsets[:]))
         nc.vector.tensor_copy(planes[:, :J].bitcast(I32), got_s[:].bitcast(I32))
         for r in range(1, 4):
-            nc.scalar.dma_start(out=planes[r:P:32, :].bitcast(I32), in_=planes[8 * r : P : 32, :].bitcast(I32))
-        wh4_last = tile([P, P], U16, "wh4_last", "got_s")
-        nc.scalar.copy(out=wh4_last[:], in_=wh4_sets[:, :, PACK - 1])
-        wh4_codes = [wh4_w[:, t * P : (t + 1) * P] for t in range(PACK - 1)] + [wh4_last[:]]
+            nc.sync.dma_start(out=planes[r:P:32, :].bitcast(I32), in_=planes[8 * r : P : 32, :].bitcast(I32))
         wg_s, wh4_s = planes[:, J : J + N], planes[:, J + N :]
 
         halves = [slice(h * HALF, (h + 1) * HALF) for h in range(J // HALF)]
@@ -103,7 +99,7 @@ def tile_list_hwayt_dl_reluP_kernel(
         make_identity(nc, ident[:])
 
         r_rows = rT.rearrange("(p t) c -> t p c", t=PACK)
-        r_tags = ("wh4_raw", "tab_w", "whd_raw", "whd_bf0")
+        r_tags = ("got_s", "tab_w", "whd_raw", "whd_bf0")
         r_tab = []
         for t in range(PACK):
             r_t = tile([P, T], F32, f"r_tab{t}", r_tags[t])
@@ -134,21 +130,22 @@ def tile_list_hwayt_dl_reluP_kernel(
             for dst, offset, sign in reads:
                 nc.scalar.activation(dst[:, halves[h]], ga[:], ACT.Sigmoid, bias=offset[:, t : t + 1], scale=sign)
 
-        def transform(t, h):
+        def transform(t, h, which=(0, 1)):
             cols = slice(t * P, (t + 1) * P)
-            ha = psum.tile([P, HALF], F32, name="ha", tag=f"bank{2 * ((t + 1) % PACK) + h}")
+            if 0 in which:
+                sums[t, h] = psum.tile([P, HALF], F32, name="ha", tag=f"bank{2 * ((t + 1) % PACK) + h}")
             passes = [
-                (wh4_codes[t].bitcast(U8).bitcast(FP4X4), wh4_s[:, cols]),
+                (wh4_w[:, cols].bitcast(U8).bitcast(FP4X4), wh4_s[:, cols]),
                 (whd_w[:, cols].bitcast(FP8X4), whd_s[:, cols]),
             ]
             if t > 0:
                 passes = passes[::-1]
-            for i, (codes, scales) in enumerate(passes):
+            for i in which:
+                codes, scales = passes[i]
                 nc.tensor.matmul_mx(
-                    out=ha[:], lhsT=codes, lhsT_scale=scales,
+                    out=sums[t, h][:], lhsT=codes, lhsT_scale=scales,
                     rhs=got_w[h][:].bitcast(FP8X4), rhs_scale=planes[:, halves[h]], start=i == 0, stop=i == 1,
                 )
-            sums[t, h] = ha
 
         def gated(t, h):
             behind = {(0, 0): "made00", (1, 0): "carry0", (2, 0): r_tags[0], (2, 1): "carry1", (3, 0): r_tags[1]}
@@ -200,11 +197,14 @@ def tile_list_hwayt_dl_reluP_kernel(
 
         for h in range(2):
             gates(0, h)
-            transform(0, h)
+        for which in range(2):
+            for h in range(2):
+                transform(0, h, (which,))
+        gates(1, 0)
         for h in range(2):
             gated(0, h)
         for t in range(1, PACK):
-            for h in range(2):
+            for h in range(int(t == 1), 2):
                 gates(t, h)
             for h in range(2):
                 transform(t, h)
@@ -271,8 +271,7 @@ def tile_list_hwayt_dl_reluP_kernel(
             if i % 2 == 1:
                 nc.sync.dma_start(out=y_rows[last][:, halves[i // 2]], in_=y[last][:, halves[i // 2]])
         round_late(nc.vector.tensor_copy, *spans[-2])
-        finish(0, HALF)
-        for lo, hi in spans[2:]:
+        for lo, hi in ((0, SHARE // 2), (SHARE // 2, SHARE), (SHARE, J)):
             finish(lo, hi)
         for r in range(4):
             (nc.sync, nc.scalar)[r % 2].dma_start(out=out_2[0, r:16:4, :].bitcast(I32), in_=y_s[r:P:32, :].bitcast(I32))

@@ -19,10 +19,15 @@ ALU = mybir.AluOpType
 
 P = 128
 PACK = 4
+QUADRANT = 32
+BLOCK = 8
+STRIPE = 16
 HALF = 512
 SHARE = 768
 PIECE = 256
-CUT = 768
+
+ADDED = ((0, 0), (0, 1), (1, 0), (1, 1), (2, 0))
+GATE_BANKS = ((0, 1), (7, 2), (3, 2), (3, 2))
 
 
 def tile_list_hwayt_dl_reluP_kernel(
@@ -36,8 +41,8 @@ def tile_list_hwayt_dl_reluP_kernel(
         def tile(shape, dtype, name, tag=None):
             return keep.tile(shape, dtype, name=name, tag=tag or name, align_bytes=64)
 
-        offsets = keep.tile([P, J // 16], U16, name="offsets")
-        nc.sync.dma_start(offsets[:], offs)
+        def listed(lo, hi):
+            return offsets[:, lo // STRIPE : hi // STRIPE]
 
         tab_s = tile([P, T], U8, "tab_s")
         w_s_raw = tile([P, 2 * N], U8, "w_s_raw")
@@ -48,15 +53,15 @@ def tile_list_hwayt_dl_reluP_kernel(
         nc.sync.dma_start(out=wg_raw[:].bitcast(I32), in_=wg_words[0].rearrange("p n i -> p (n i)").bitcast(I32))
         wh4_raw = tile([P, N], U16, "wh4_raw")
         nc.sync.dma_start(out=wh4_raw[:].bitcast(I32), in_=wh4_words[0].bitcast(I32))
+        offsets = keep.tile([P, J // STRIPE], U16, name="offsets")
+        nc.sync.dma_start(offsets[:], offs)
         for w, rows in enumerate((wg_scales, wh4_scales)):
-            nc.sync.dma_start(out=w_s_raw[0:P:8, w * N : (w + 1) * N].bitcast(I32), in_=rows[0].bitcast(I32))
-        tab_w = tile([P, T], U32, "tab_w")
-        tab_rows = tab_words[0].rearrange("p n i -> p (n i)").bitcast(I32)
-        nc.sync.dma_start(out=tab_w[:, :CUT].bitcast(I32), in_=tab_rows[:, :CUT])
-        nc.sync.dma_start(out=tab_s[0:P:8, :].bitcast(I32), in_=tab_scales[0].bitcast(I32))
-        nc.sync.dma_start(out=tab_w[:, CUT:].bitcast(I32), in_=tab_rows[:, CUT:])
+            nc.sync.dma_start(out=w_s_raw[0:P:BLOCK, w * N : (w + 1) * N].bitcast(I32), in_=rows[0].bitcast(I32))
         bias = tile([P, PACK], F32, "bias")
         nc.sync.dma_start(out=bias[:], in_=bg.rearrange("(p t) -> p t", t=PACK))
+        nc.sync.dma_start(out=tab_s[0:P:BLOCK, :].bitcast(I32), in_=tab_scales[0].bitcast(I32))
+        tab_w = tile([P, T], U32, "tab_w")
+        nc.sync.dma_start(out=tab_w[:].bitcast(I32), in_=tab_words[0].rearrange("p n i -> p (n i)").bitcast(I32))
         whd_raw = tile([P, PACK, N], F32, "whd_raw")
         nc.sync.dma_start(out=whd_raw[:], in_=whd.rearrange("(p i) n -> p i n", i=PACK))
 
@@ -66,24 +71,24 @@ def tile_list_hwayt_dl_reluP_kernel(
         wh4_w = tile([P, N], U16, "wh4_w")
         for dealt, raw in ((wg_w, wg_raw), (wh4_w, wh4_raw)):
             nc.scalar.copy(out=dealt[:].rearrange("p (t m) -> p m t", t=PACK), in_=raw[:].rearrange("p (m t) -> p m t", t=PACK))
-        planes = tile([P, J + 2 * N], U8, "planes")
+        scales = tile([P, J + 2 * N], U8, "scales")
         nc.vector.tensor_copy(
-            out=planes[:, J:].rearrange("p (w t m) -> p w t m", w=2, t=PACK),
+            out=scales[:, J:].rearrange("p (w t m) -> p w t m", w=2, t=PACK),
             in_=w_s_raw[:].rearrange("p (w m t) -> p w t m", w=2, t=PACK),
         )
         got_s = tile([P, J], U8, "got_s")
         nc.vector.tensor_copy(got_s[:], tab_s[:].indirect(offsets[:]))
-        nc.vector.tensor_copy(planes[:, :J].bitcast(I32), got_s[:].bitcast(I32))
-        for r in range(1, 4):
-            nc.sync.dma_start(out=planes[r:P:32, :].bitcast(I32), in_=planes[8 * r : P : 32, :].bitcast(I32))
-        wg_s, wh4_s = planes[:, J : J + N], planes[:, J + N :]
+        nc.vector.tensor_copy(scales[:, :J].bitcast(I32), got_s[:].bitcast(I32))
+        for r in range(1, QUADRANT // BLOCK):
+            nc.sync.dma_start(out=scales[r:P:QUADRANT, :].bitcast(I32), in_=scales[BLOCK * r : P : QUADRANT, :].bitcast(I32))
+        wg_s, wh4_s = scales[:, J : J + N], scales[:, J + N :]
 
         halves = [slice(h * HALF, (h + 1) * HALF) for h in range(J // HALF)]
         got_w = []
-        for h in range(2):
-            w_h = tile([P, HALF], U32, f"got_w{h}")
-            nc.vector.tensor_copy(w_h[:], tab_w[:].indirect(offsets[:, h * 32 : (h + 1) * 32]))
-            got_w.append(w_h)
+        for h, entries in enumerate(halves):
+            got_half = tile([P, HALF], U32, f"got_w{h}")
+            nc.vector.tensor_copy(got_half[:], tab_w[:].indirect(listed(entries.start, entries.stop)))
+            got_w.append(got_half)
         whd_w = tile([P, N], U32, "whd_w")
         whd_s = tile([P, N], U8, "whd_s")
         for u in range(2):
@@ -102,38 +107,37 @@ def tile_list_hwayt_dl_reluP_kernel(
         r_tags = ("got_s", "tab_w", "whd_raw", "whd_bf0")
         r_tab = []
         for t in range(PACK):
-            r_t = tile([P, T], F32, f"r_tab{t}", r_tags[t])
-            nc.sync.dma_start(out=r_t[:], in_=r_rows[t])
-            r_tab.append(r_t)
+            r_set = tile([P, T], F32, f"r_tab{t}", r_tags[t])
+            nc.sync.dma_start(out=r_set[:], in_=r_rows[t])
+            r_tab.append(r_set)
 
         y_lo = keep.tile([P, 2, J], F32, name="y_lo")
         y_hi = keep.tile([P, 2, J], F32, name="y_hi")
         y = [y_lo[:, 0, :], y_lo[:, 1, :], y_hi[:, 0, :], y_hi[:, 1, :]]
         y_rows = out_0.rearrange("(p t) j -> t p j", t=PACK)
-        gate, carry, made, sums, parts = {}, {}, {}, {}, {}
-        on_tensor = ((0, 0), (0, 1), (1, 0), (1, 1), (2, 0))
+        gate, carry, ha, made, kept = {}, {}, {}, {}, {}
 
-        def gates(t, h):
+        def gate_pass(t, h):
             cols = slice(t * P, (t + 1) * P)
             if h == 0:
                 carry[t] = tile([P, J], F32, f"carry{t}")
-                if (t, h) in on_tensor:
+                if (t, h) in ADDED:
                     gate[t] = keep.tile([P, J], F32, name=f"gate{t}")
-            ga = psum.tile([P, HALF], F32, name="ga", tag=f"bank{((0, 1), (7, 2), (3, 2), (3, 2))[t][h]}")
+            ga = psum.tile([P, HALF], F32, name="ga", tag=f"bank{GATE_BANKS[t][h]}")
             nc.tensor.matmul_mx(
                 out=ga[:], lhsT=wg_w[:, cols].bitcast(FP8X4), lhsT_scale=wg_s[:, cols],
-                rhs=got_w[h][:].bitcast(FP8X4), rhs_scale=planes[:, halves[h]], start=True, stop=True,
+                rhs=got_w[h][:].bitcast(FP8X4), rhs_scale=scales[:, halves[h]], start=True, stop=True,
             )
             reads = [(carry[t], neg_bias, -1.0)]
-            if (t, h) in on_tensor:
+            if (t, h) in ADDED:
                 reads.insert(int((t, h) == (0, 1)), (gate[t], bias, 1.0))
             for dst, offset, sign in reads:
                 nc.scalar.activation(dst[:, halves[h]], ga[:], ACT.Sigmoid, bias=offset[:, t : t + 1], scale=sign)
 
-        def transform(t, h, which=(0, 1)):
+        def ha_passes(t, h, which=(0, 1)):
             cols = slice(t * P, (t + 1) * P)
             if 0 in which:
-                sums[t, h] = psum.tile([P, HALF], F32, name="ha", tag=f"bank{2 * ((t + 1) % PACK) + h}")
+                ha[t, h] = psum.tile([P, HALF], F32, name="ha", tag=f"bank{2 * ((t + 1) % PACK) + h}")
             passes = [
                 (wh4_w[:, cols].bitcast(U8).bitcast(FP4X4), wh4_s[:, cols]),
                 (whd_w[:, cols].bitcast(FP8X4), whd_s[:, cols]),
@@ -141,46 +145,50 @@ def tile_list_hwayt_dl_reluP_kernel(
             if t > 0:
                 passes = passes[::-1]
             for i in which:
-                codes, scales = passes[i]
+                codes, code_scales = passes[i]
                 nc.tensor.matmul_mx(
-                    out=sums[t, h][:], lhsT=codes, lhsT_scale=scales,
-                    rhs=got_w[h][:].bitcast(FP8X4), rhs_scale=planes[:, halves[h]], start=i == 0, stop=i == 1,
+                    out=ha[t, h][:], lhsT=codes, lhsT_scale=code_scales,
+                    rhs=got_w[h][:].bitcast(FP8X4), rhs_scale=scales[:, halves[h]], start=i == 0, stop=i == 1,
                 )
 
-        def gated(t, h):
-            behind = {(0, 0): "made00", (1, 0): "carry0", (2, 0): r_tags[0], (2, 1): "carry1", (3, 0): r_tags[1]}
-            if (t, h) in behind:
-                made[t, h] = tile([P, J], F32, f"made{t}_{h}", behind[t, h])
+        def read_ha(t, h):
+            buffers = {(0, 0): "made00", (1, 0): "carry0", (2, 0): r_tags[0], (2, 1): "carry1", (3, 0): r_tags[1]}
+            if (t, h) in buffers:
+                made[t, h] = tile([P, J], F32, f"made{t}_{h}", buffers[t, h])
             else:
                 made[t, h] = made[t, 0]
-            if (t, h) in on_tensor:
+            if (t, h) in ADDED:
                 nc.vector.scalar_tensor_tensor(
-                    out=made[t, h][:, halves[h]], in0=sums[t, h][:], scalar=0.0, in1=gate[t][:, halves[h]], op0=ALU.max, op1=ALU.mult
+                    out=made[t, h][:, halves[h]], in0=ha[t, h][:], scalar=0.0, in1=gate[t][:, halves[h]], op0=ALU.max, op1=ALU.mult
                 )
             else:
                 nc.vector.scalar_tensor_tensor(
-                    out=made[t, h][:, halves[h]], in0=carry[t][:, halves[h]], scalar=1.0, in1=sums[t, h][:], op0=ALU.subtract, op1=ALU.mult
+                    out=made[t, h][:, halves[h]], in0=carry[t][:, halves[h]], scalar=1.0, in1=ha[t, h][:], op0=ALU.subtract, op1=ALU.mult
                 )
 
-        def new_part(t, lo, hi, tag):
-            parts[t, lo, hi] = tile([P, hi - lo], F32, f"kept{t}_{lo}", tag)
+        def new_kept(t, lo, hi, tag):
+            kept[t, lo, hi] = tile([P, hi - lo], F32, f"kept{t}_{lo}", tag)
 
-        def part(t, lo, hi):
-            start, end = [(a, b) for u, a, b in parts if u == t and a <= lo and hi <= b][0]
-            return parts[t, start, end][:, lo - start : hi - start]
+        def kept_cols(t, lo, hi):
+            start, end = [(a, b) for u, a, b in kept if u == t and a <= lo and hi <= b][0]
+            return kept[t, start, end][:, lo - start : hi - start]
 
-        def kept(t, lo, hi):
-            nc.vector.tensor_tensor(part(t, lo, hi), r_tab[t][:].indirect(offsets[:, lo // 16 : hi // 16]), carry[t][:, lo:hi], ALU.mult)
+        def gather_r(t, lo, hi):
+            nc.vector.tensor_tensor(kept_cols(t, lo, hi), r_tab[t][:].indirect(listed(lo, hi)), carry[t][:, lo:hi], ALU.mult)
 
         def blend(t, lo, hi):
             nc.vector.scalar_tensor_tensor(
-                out=y[t][:, lo:hi], in0=made[t, lo // HALF][:, lo:hi], scalar=0.0, in1=part(t, lo, hi), op0=ALU.min, op1=ALU.subtract, reverse1=True
+                out=y[t][:, lo:hi], in0=made[t, lo // HALF][:, lo:hi], scalar=0.0, in1=kept_cols(t, lo, hi),
+                op0=ALU.min, op1=ALU.subtract, reverse1=True,
             )
 
         def turn(dst, src, start, stop):
             width = dst.shape[1]
             for c in range(0, width, P):
-                nc.tensor.matmul(dst[:, c : c + P], src[:, c : c + P], ident[:], start=start and c == 0, stop=stop and c == width - P, is_transpose=True)
+                nc.tensor.matmul(
+                    dst[:, c : c + P], src[:, c : c + P], ident[:],
+                    start=start and c == 0, stop=stop and c == width - P, is_transpose=True,
+                )
 
         def open_sum(t, lo, hi, bank):
             turned = psum.tile([P, hi - lo], F32, name="turned", tag=f"bank{bank}")
@@ -188,90 +196,96 @@ def tile_list_hwayt_dl_reluP_kernel(
             return turned
 
         def close_sum(t, lo, hi, turned, bank):
-            turn(turned[:], part(t, lo, hi), False, True)
-            staged = keep.tile([P, hi - lo], F32, name=f"staged{t}_{lo}", tag=f"staged{t}_{lo}", align_bytes=64)
+            turn(turned[:], kept_cols(t, lo, hi), False, True)
+            staged = tile([P, hi - lo], F32, f"staged{t}_{lo}")
             nc.scalar.copy(staged[:], turned[:])
             back = psum.tile([P, hi - lo], F32, name="back", tag=f"bank{bank}")
             turn(back[:], staged[:], True, True)
             nc.scalar.copy(y[t][:, lo:hi], back[:])
 
         for h in range(2):
-            gates(0, h)
+            gate_pass(0, h)
         for which in range(2):
             for h in range(2):
-                transform(0, h, (which,))
-        gates(1, 0)
+                ha_passes(0, h, (which,))
+        gate_pass(1, 0)
         for h in range(2):
-            gated(0, h)
+            read_ha(0, h)
         for t in range(1, PACK):
             for h in range(int(t == 1), 2):
-                gates(t, h)
+                gate_pass(t, h)
             for h in range(2):
-                transform(t, h)
-        first, second = slice(0, SHARE), slice(SHARE, J)
-        woven = {SHARE: keep.tile([P, J - SHARE, PACK], BF16, name="y_bf_rest", align_bytes=64)}
+                ha_passes(t, h)
 
-        def y_bf(lo, hi):
+        shared, rest = slice(0, SHARE), slice(SHARE, J)
+        woven = {SHARE: keep.tile([P, J - SHARE, PACK], BF16, name="woven_rest", align_bytes=64)}
+
+        def woven_cols(lo, hi):
             base = SHARE if lo >= SHARE else 0
             return woven[base][:, lo - base : hi - base, :]
 
-        def round_early(cols):
-            nc.scalar.copy(out=y_bf(cols.start, cols.stop)[:, :, 0:2], in_=y_lo[:, :, cols].rearrange("p t j -> p j t"))
+        def round_lo(cols):
+            nc.scalar.copy(out=woven_cols(cols.start, cols.stop)[:, :, 0:2], in_=y_lo[:, :, cols].rearrange("p t j -> p j t"))
 
+        def round_hi(copy, lo, hi):
+            copy(out=woven_cols(lo, hi)[:, :, 2:4], in_=y_hi[:, :, lo:hi].rearrange("p t j -> p j t"))
+
+        new_kept(0, 0, J, "kept0_0")
+        gather_r(0, 0, J)
+        for t, h in ((1, 0), (1, 1), (2, 0)):
+            read_ha(t, h)
+        nc.gpsimd.tensor_tensor(y[0][:, shared], kept_cols(0, 0, SHARE), made[0, 0][:, shared], ALU.add)
+        close_sum(0, SHARE, J, open_sum(0, SHARE, J, 3), 2)
+        rest_of_set_1 = open_sum(1, SHARE, J, 4)
         quarters = ((0, HALF // 2), (HALF // 2, HALF))
-        behind_gather = (((1, 0), (1, 1), (2, 0)), ((2, 1), (3, 0), (3, 1)), ())
-        gathers = (((0, J),), ((SHARE, J), (0, SHARE)), ((0, HALF), (HALF, J)))
-        for t in range(PACK - 1):
-            for lo, hi in gathers[t]:
-                new_part(t, lo, hi, f"kept{t}_{lo}")
-                kept(t, lo, hi)
-            if t == 1:
-                close_sum(t, SHARE, J, rest, 4)
-                round_early(second)
-                woven[0] = keep.tile([P, SHARE, PACK], BF16, name="y_bf", tag=f"staged1_{SHARE}", align_bytes=64)
-            if t == 2:
-                for i, (lo, hi) in enumerate(quarters):
-                    close_sum(t, lo, hi, opened[i], 2 + i)
-            for u, h in behind_gather[t]:
-                gated(u, h)
-            if t == 0:
-                nc.gpsimd.tensor_tensor(y[t][:, first], part(t, 0, SHARE), made[t, 0][:, first], ALU.add)
-                close_sum(t, SHARE, J, open_sum(t, SHARE, J, 3), 2)
-                rest = open_sum(1, SHARE, J, 4)
-                opened = [open_sum(2, lo, hi, 5 + i) for i, (lo, hi) in enumerate(quarters)]
-            if t == 1:
-                for cols in (slice(0, SHARE // 2), slice(SHARE // 2, SHARE)):
-                    nc.gpsimd.tensor_tensor(y[t][:, cols], part(t, cols.start, cols.stop), made[t, 0][:, cols], ALU.add)
-                    round_early(cols)
-            if t == 2:
-                blend(t, HALF, J)
-            nc.sync.dma_start(out=y_rows[t], in_=y[t])
+        quarters_of_set_2 = [open_sum(2, lo, hi, 5 + i) for i, (lo, hi) in enumerate(quarters)]
+        nc.sync.dma_start(out=y_rows[0], in_=y[0])
+
+        for lo, hi in ((SHARE, J), (0, SHARE)):
+            new_kept(1, lo, hi, f"kept1_{lo}")
+            gather_r(1, lo, hi)
+        close_sum(1, SHARE, J, rest_of_set_1, 4)
+        round_lo(rest)
+        woven[0] = tile([P, SHARE, PACK], BF16, "woven_shared", f"staged1_{SHARE}")
+        for t, h in ((2, 1), (3, 0), (3, 1)):
+            read_ha(t, h)
+        for cols in (slice(0, SHARE // 2), slice(SHARE // 2, SHARE)):
+            nc.gpsimd.tensor_tensor(y[1][:, cols], kept_cols(1, cols.start, cols.stop), made[1, 0][:, cols], ALU.add)
+            round_lo(cols)
+        nc.sync.dma_start(out=y_rows[1], in_=y[1])
+
+        for lo, hi in ((0, HALF), (HALF, J)):
+            new_kept(2, lo, hi, f"kept2_{lo}")
+            gather_r(2, lo, hi)
+        for i, (lo, hi) in enumerate(quarters):
+            close_sum(2, lo, hi, quarters_of_set_2[i], 2 + i)
+        blend(2, HALF, J)
+        nc.sync.dma_start(out=y_rows[2], in_=y[2])
 
         y_w = keep.tile([P, J], U32, name="y_w", align_bytes=64)
         y_s = keep.tile([P, J], U8, name="y_s", align_bytes=64)
         words_out = out_1[0].rearrange("p j i -> p (j i)").bitcast(I32)
         last = PACK - 1
-        spans = [(lo, lo + PIECE) for lo in range(0, J, PIECE)]
+        pieces = [(lo, lo + PIECE) for lo in range(0, J, PIECE)]
+        on_vector = len(pieces) - 2
 
-        def round_late(copy, lo, hi):
-            copy(out=y_bf(lo, hi)[:, :, 2:4], in_=y_hi[:, :, lo:hi].rearrange("p t j -> p j t"))
-
-        def finish(lo, hi):
-            nc.vector.quantize_mx(out=y_w[:, lo:hi].bitcast(FP8X4), scales=y_s[:, lo:hi], in_=y_bf(lo, hi).rearrange("p j t -> p (j t)"))
-            nc.sync.dma_start(out=words_out[:, lo:hi], in_=y_w[:, lo:hi].bitcast(I32))
-
-        new_part(last, 0, J, "carry1")
-        kept(last, *spans[0])
-        for i, (lo, hi) in enumerate(spans):
-            if i + 1 < len(spans):
-                kept(last, *spans[i + 1])
+        new_kept(last, 0, J, "carry1")
+        gather_r(last, *pieces[0])
+        for i, (lo, hi) in enumerate(pieces):
+            if i + 1 < len(pieces):
+                gather_r(last, *pieces[i + 1])
             blend(last, lo, hi)
-            if i != len(spans) - 2:
-                round_late(nc.scalar.copy, lo, hi)
-            if i % 2 == 1:
-                nc.sync.dma_start(out=y_rows[last][:, halves[i // 2]], in_=y[last][:, halves[i // 2]])
-        round_late(nc.vector.tensor_copy, *spans[-2])
+            if i != on_vector:
+                round_hi(nc.scalar.copy, lo, hi)
+            if hi % HALF == 0:
+                nc.sync.dma_start(out=y_rows[last][:, hi - HALF : hi], in_=y[last][:, hi - HALF : hi])
+        round_hi(nc.vector.tensor_copy, *pieces[on_vector])
         for lo, hi in ((0, SHARE // 2), (SHARE // 2, SHARE), (SHARE, J)):
-            finish(lo, hi)
-        for r in range(4):
-            (nc.sync, nc.scalar)[r % 2].dma_start(out=out_2[0, r:16:4, :].bitcast(I32), in_=y_s[r:P:32, :].bitcast(I32))
+            nc.vector.quantize_mx(
+                out=y_w[:, lo:hi].bitcast(FP8X4), scales=y_s[:, lo:hi], in_=woven_cols(lo, hi).rearrange("p j t -> p (j t)")
+            )
+            nc.sync.dma_start(out=words_out[:, lo:hi], in_=y_w[:, lo:hi].bitcast(I32))
+        for r in range(QUADRANT // BLOCK):
+            (nc.sync, nc.scalar)[r % 2].dma_start(
+                out=out_2[0, r :: QUADRANT // BLOCK, :].bitcast(I32), in_=y_s[r:P:QUADRANT, :].bitcast(I32)
+            )

@@ -25,6 +25,7 @@ STRIPE = 16
 HALF = 512
 SHARE = 768
 PIECE = 256
+CUT = 512
 
 ADDED = ((0, 0), (0, 1), (1, 0), (1, 1), (2, 0))
 GATE_BANKS = ((0, 1), (7, 2), (3, 2), (3, 2))
@@ -57,16 +58,16 @@ def tile_list_hwayt_dl_reluP_kernel(
         nc.sync.dma_start(offsets[:], offs)
         for w, rows in enumerate((wg_scales, wh4_scales)):
             nc.sync.dma_start(out=w_s_raw[0:P:BLOCK, w * N : (w + 1) * N].bitcast(I32), in_=rows[0].bitcast(I32))
+        tab_w = tile([P, T], U32, "tab_w")
+        tab_rows = tab_words[0].rearrange("p n i -> p (n i)").bitcast(I32)
+        nc.sync.dma_start(out=tab_w[:, :CUT].bitcast(I32), in_=tab_rows[:, :CUT])
+        nc.sync.dma_start(out=tab_s[0:P:BLOCK, :].bitcast(I32), in_=tab_scales[0].bitcast(I32))
+        nc.sync.dma_start(out=tab_w[:, CUT:].bitcast(I32), in_=tab_rows[:, CUT:])
         bias = tile([P, PACK], F32, "bias")
         nc.sync.dma_start(out=bias[:], in_=bg.rearrange("(p t) -> p t", t=PACK))
-        nc.sync.dma_start(out=tab_s[0:P:BLOCK, :].bitcast(I32), in_=tab_scales[0].bitcast(I32))
-        tab_w = tile([P, T], U32, "tab_w")
-        nc.sync.dma_start(out=tab_w[:].bitcast(I32), in_=tab_words[0].rearrange("p n i -> p (n i)").bitcast(I32))
         whd_raw = tile([P, PACK, N], F32, "whd_raw")
         nc.sync.dma_start(out=whd_raw[:], in_=whd.rearrange("(p i) n -> p i n", i=PACK))
 
-        neg_bias = tile([P, PACK], F32, "neg_bias")
-        nc.vector.tensor_scalar(neg_bias[:], bias[:], -1.0, None, ALU.mult)
         wg_w = tile([P, N], U32, "wg_w")
         wh4_w = tile([P, N], U16, "wh4_w")
         for dealt, raw in ((wg_w, wg_raw), (wh4_w, wh4_raw)):
@@ -89,6 +90,8 @@ def tile_list_hwayt_dl_reluP_kernel(
             got_half = tile([P, HALF], U32, f"got_w{h}")
             nc.vector.tensor_copy(got_half[:], tab_w[:].indirect(listed(entries.start, entries.stop)))
             got_w.append(got_half)
+        neg_bias = tile([P, PACK], F32, "neg_bias")
+        nc.vector.tensor_scalar(neg_bias[:], bias[:], -1.0, None, ALU.mult)
         whd_w = tile([P, N], U32, "whd_w")
         whd_s = tile([P, N], U8, "whd_s")
         for u in range(2):

@@ -25,7 +25,6 @@ STRIPE = 16
 HALF = 512
 SHARE = 768
 PIECE = 256
-CUT = 512
 
 ADDED = ((0, 0), (0, 1), (1, 0), (1, 1), (2, 0))
 GATE_BANKS = ((0, 1), (7, 2), (3, 2), (3, 2))
@@ -47,7 +46,7 @@ def tile_list_hwayt_dl_reluP_kernel(
 
         tab_s = tile([P, T], U8, "tab_s")
         w_s_raw = tile([P, 2 * N], U8, "w_s_raw")
-        nc.gpsimd.memset(w_s_raw[:].bitcast(I32), 0)
+        nc.vector.memset(w_s_raw[:].bitcast(I32), 0)
         nc.vector.memset(tab_s[:].bitcast(I32), 0)
 
         wg_raw = tile([P, N], U32, "wg_raw")
@@ -58,13 +57,11 @@ def tile_list_hwayt_dl_reluP_kernel(
         nc.sync.dma_start(offsets[:], offs)
         for w, rows in enumerate((wg_scales, wh4_scales)):
             nc.sync.dma_start(out=w_s_raw[0:P:BLOCK, w * N : (w + 1) * N].bitcast(I32), in_=rows[0].bitcast(I32))
-        tab_w = tile([P, T], U32, "tab_w")
-        tab_rows = tab_words[0].rearrange("p n i -> p (n i)").bitcast(I32)
-        nc.sync.dma_start(out=tab_w[:, :CUT].bitcast(I32), in_=tab_rows[:, :CUT])
-        nc.sync.dma_start(out=tab_s[0:P:BLOCK, :].bitcast(I32), in_=tab_scales[0].bitcast(I32))
-        nc.sync.dma_start(out=tab_w[:, CUT:].bitcast(I32), in_=tab_rows[:, CUT:])
         bias = tile([P, PACK], F32, "bias")
         nc.sync.dma_start(out=bias[:], in_=bg.rearrange("(p t) -> p t", t=PACK))
+        nc.sync.dma_start(out=tab_s[0:P:BLOCK, :].bitcast(I32), in_=tab_scales[0].bitcast(I32))
+        tab_w = tile([P, T], U32, "tab_w")
+        nc.sync.dma_start(out=tab_w[:].bitcast(I32), in_=tab_words[0].rearrange("p n i -> p (n i)").bitcast(I32))
         whd_raw = tile([P, PACK, N], F32, "whd_raw")
         nc.sync.dma_start(out=whd_raw[:], in_=whd.rearrange("(p i) n -> p i n", i=PACK))
 

from contextlib import ExitStack

import concourse.mybir as mybir
from concourse.masks import make_identity

K, N, T, J = 512, 512, 4096, 1024
FLOPS = 3 * 2 * K * N * J

F32 = mybir.dt.float32
BF16 = mybir.dt.bfloat16
I32 = mybir.dt.int32
U32 = mybir.dt.uint32
U16 = mybir.dt.uint16
U8 = mybir.dt.uint8
FP8X4 = mybir.dt.float8_e4m3fn_x4
FP4X4 = mybir.dt.float4_e2m1fn_x4
ACT = mybir.ActivationFunctionType
ALU = mybir.AluOpType

P = 128
PACK = 4
QUADRANT = 32
BLOCK = 8
STRIPE = 16
HALF = 512
SHARE = 768
PIECE = 256

ADDED = ((0, 0), (0, 1), (1, 0), (1, 1), (2, 0))
GATE_BANKS = ((0, 1), (7, 2), (3, 2), (3, 2))


def tile_list_hwayt_dl_reluP_kernel(
    tc, tab_words, tab_scales, wg_words, wg_scales, wh4_words, wh4_scales, whd, bg, rT, offs, out_0, out_1, out_2
):
    nc = tc.nc
    with ExitStack() as ctx:
        keep = ctx.enter_context(tc.tile_pool(name="keep", bufs=1))
        psum = ctx.enter_context(tc.psum_pool(name="psum", bufs=1))

        def tile(shape, dtype, name, tag=None):
            return keep.tile(shape, dtype, name=name, tag=tag or name, align_bytes=64)

        def listed(lo, hi):
            return offsets[:, lo // STRIPE : hi // STRIPE]

        tab_s = tile([P, T], U8, "tab_s")
        w_s_raw = tile([P, 2 * N], U8, "w_s_raw")
        nc.vector.memset(w_s_raw[:].bitcast(I32), 0)
        nc.vector.memset(tab_s[:].bitcast(I32), 0)

        wg_raw = tile([P, N], U32, "wg_raw")
        nc.sync.dma_start(out=wg_raw[:].bitcast(I32), in_=wg_words[0].rearrange("p n i -> p (n i)").bitcast(I32))
        wh4_raw = tile([P, N], U16, "wh4_raw")
        nc.sync.dma_start(out=wh4_raw[:].bitcast(I32), in_=wh4_words[0].bitcast(I32))
        offsets = keep.tile([P, J // STRIPE], U16, name="offsets")
        nc.sync.dma_start(offsets[:], offs)
        for w, rows in enumerate((wg_scales, wh4_scales)):
            nc.sync.dma_start(out=w_s_raw[0:P:BLOCK, w * N : (w + 1) * N].bitcast(I32), in_=rows[0].bitcast(I32))
        bias = tile([P, PACK], F32, "bias")
        nc.sync.dma_start(out=bias[:], in_=bg.rearrange("(p t) -> p t", t=PACK))
        nc.sync.dma_start(out=tab_s[0:P:BLOCK, :].bitcast(I32), in_=tab_scales[0].bitcast(I32))
        tab_w = tile([P, T], U32, "tab_w")
        nc.sync.dma_start(out=tab_w[:].bitcast(I32), in_=tab_words[0].rearrange("p n i -> p (n i)").bitcast(I32))
        whd_raw = tile([P, PACK, N], F32, "whd_raw")
        nc.sync.dma_start(out=whd_raw[:], in_=whd.rearrange("(p i) n -> p i n", i=PACK))

        wg_w = tile([P, N], U32, "wg_w")
        wh4_w = tile([P, N], U16, "wh4_w")
        for dealt, raw in ((wg_w, wg_raw), (wh4_w, wh4_raw)):
            nc.scalar.copy(out=dealt[:].rearrange("p (t m) -> p m t", t=PACK), in_=raw[:].rearrange("p (m t) -> p m t", t=PACK))
        scales = tile([P, J + 2 * N], U8, "scales")
        nc.vector.tensor_copy(
            out=scales[:, J:].rearrange("p (w t m) -> p w t m", w=2, t=PACK),
            in_=w_s_raw[:].rearrange("p (w m t) -> p w t m", w=2, t=PACK),
        )
        got_s = tile([P, J], U8, "got_s")
        nc.vector.tensor_copy(got_s[:], tab_s[:].indirect(offsets[:]))
        nc.vector.tensor_copy(scales[:, :J].bitcast(I32), got_s[:].bitcast(I32))
        for r in range(1, QUADRANT // BLOCK):
            nc.sync.dma_start(out=scales[r:P:QUADRANT, :].bitcast(I32), in_=scales[BLOCK * r : P : QUADRANT, :].bitcast(I32))
        wg_s, wh4_s = scales[:, J : J + N], scales[:, J + N :]

        halves = [slice(h * HALF, (h + 1) * HALF) for h in range(J // HALF)]
        got_w = []
        for h, entries in enumerate(halves):
            got_half = tile([P, HALF], U32, f"got_w{h}")
            nc.vector.tensor_copy(got_half[:], tab_w[:].indirect(listed(entries.start, entries.stop)))
            got_w.append(got_half)
        neg_bias = tile([P, PACK], F32, "neg_bias")
        nc.vector.tensor_scalar(neg_bias[:], bias[:], -1.0, None, ALU.mult)
        whd_w = tile([P, N], U32, "whd_w")
        whd_s = tile([P, N], U8, "whd_s")
        for u in range(2):
            whd_bf = tile([P, PACK * N // 2], BF16, f"whd_bf{u}")
            nc.vector.tensor_copy(
                out=whd_bf[:].rearrange("p (t m i) -> p m t i", t=2, i=PACK),
                in_=whd_raw[:].rearrange("p i (m t) -> p m t i", t=PACK)[:, :, 2 * u : 2 * u + 2, :],
            )
            cols = slice(u * N // 2, (u + 1) * N // 2)
            nc.vector.quantize_mx(out=whd_w[:, cols].bitcast(FP8X4), scales=whd_s[:, cols], in_=whd_bf[:])

        ident = tile([P, P], F32, "ident", "whd_bf1")
        make_identity(nc, ident[:])

        r_rows = rT.rearrange("(p t) c -> t p c", t=PACK)
        r_tags = ("got_s", "tab_w", "whd_raw", "whd_bf0")
        r_tab = []
        for t in range(PACK):
            r_set = tile([P, T], F32, f"r_tab{t}", r_tags[t])
            nc.sync.dma_start(out=r_set[:], in_=r_rows[t])
            r_tab.append(r_set)

        y_lo = keep.tile([P, 2, J], F32, name="y_lo")
        y_hi = keep.tile([P, 2, J], F32, name="y_hi")
        y = [y_lo[:, 0, :], y_lo[:, 1, :], y_hi[:, 0, :], y_hi[:, 1, :]]
        y_rows = out_0.rearrange("(p t) j -> t p j", t=PACK)
        gate, carry, ha, made, kept = {}, {}, {}, {}, {}

        def gate_pass(t, h):
            cols = slice(t * P, (t + 1) * P)
            if h == 0:
                carry[t] = tile([P, J], F32, f"carry{t}")
                if (t, h) in ADDED:
                    gate[t] = keep.tile([P, J], F32, name=f"gate{t}")
            ga = psum.tile([P, HALF], F32, name="ga", tag=f"bank{GATE_BANKS[t][h]}")
            nc.tensor.matmul_mx(
                out=ga[:], lhsT=wg_w[:, cols].bitcast(FP8X4), lhsT_scale=wg_s[:, cols],
                rhs=got_w[h][:].bitcast(FP8X4), rhs_scale=scales[:, halves[h]], start=True, stop=True,
            )
            reads = [(carry[t], neg_bias, -1.0)]
            if (t, h) in ADDED:
                reads.insert(int((t, h) == (0, 1)), (gate[t], bias, 1.0))
            for dst, offset, sign in reads:
                nc.scalar.activation(dst[:, halves[h]], ga[:], ACT.Sigmoid, bias=offset[:, t : t + 1], scale=sign)

        def ha_passes(t, h, which=(0, 1)):
            cols = slice(t * P, (t + 1) * P)
            if 0 in which:
                ha[t, h] = psum.tile([P, HALF], F32, name="ha", tag=f"bank{2 * ((t + 1) % PACK) + h}")
            passes = [
                (wh4_w[:, cols].bitcast(U8).bitcast(FP4X4), wh4_s[:, cols]),
                (whd_w[:, cols].bitcast(FP8X4), whd_s[:, cols]),
            ]
            if t > 0:
                passes = passes[::-1]
            for i in which:
                codes, code_scales = passes[i]
                nc.tensor.matmul_mx(
                    out=ha[t, h][:], lhsT=codes, lhsT_scale=code_scales,
                    rhs=got_w[h][:].bitcast(FP8X4), rhs_scale=scales[:, halves[h]], start=i == 0, stop=i == 1,
                )

        def read_ha(t, h):
            buffers = {(0, 0): "made00", (1, 0): "carry0", (2, 0): r_tags[0], (2, 1): "carry1", (3, 0): r_tags[1]}
            if (t, h) in buffers:
                made[t, h] = tile([P, J], F32, f"made{t}_{h}", buffers[t, h])
            else:
                made[t, h] = made[t, 0]
            if (t, h) in ADDED:
                nc.vector.scalar_tensor_tensor(
                    out=made[t, h][:, halves[h]], in0=ha[t, h][:], scalar=0.0, in1=gate[t][:, halves[h]], op0=ALU.max, op1=ALU.mult
                )
            else:
                nc.vector.scalar_tensor_tensor(
                    out=made[t, h][:, halves[h]], in0=carry[t][:, halves[h]], scalar=1.0, in1=ha[t, h][:], op0=ALU.subtract, op1=ALU.mult
                )

        def new_kept(t, lo, hi, tag):
            kept[t, lo, hi] = tile([P, hi - lo], F32, f"kept{t}_{lo}", tag)

        def kept_cols(t, lo, hi):
            start, end = [(a, b) for u, a, b in kept if u == t and a <= lo and hi <= b][0]
            return kept[t, start, end][:, lo - start : hi - start]

        def gather_r(t, lo, hi):
            nc.vector.tensor_tensor(kept_cols(t, lo, hi), r_tab[t][:].indirect(listed(lo, hi)), carry[t][:, lo:hi], ALU.mult)

        def blend(t, lo, hi):
            nc.vector.scalar_tensor_tensor(
                out=y[t][:, lo:hi], in0=made[t, lo // HALF][:, lo:hi], scalar=0.0, in1=kept_cols(t, lo, hi),
                op0=ALU.min, op1=ALU.subtract, reverse1=True,
            )

        def turn(dst, src, start, stop):
            width = dst.shape[1]
            for c in range(0, width, P):
                nc.tensor.matmul(
                    dst[:, c : c + P], src[:, c : c + P], ident[:],
                    start=start and c == 0, stop=stop and c == width - P, is_transpose=True,
                )

        def open_sum(t, lo, hi, bank):
            turned = psum.tile([P, hi - lo], F32, name="turned", tag=f"bank{bank}")
            turn(turned[:], made[t, lo // HALF][:, lo:hi], True, False)
            return turned

        def close_sum(t, lo, hi, turned, bank):
            turn(turned[:], kept_cols(t, lo, hi), False, True)
            staged = tile([P, hi - lo], F32, f"staged{t}_{lo}")
            nc.scalar.copy(staged[:], turned[:])
            back = psum.tile([P, hi - lo], F32, name="back", tag=f"bank{bank}")
            turn(back[:], staged[:], True, True)
            nc.scalar.copy(y[t][:, lo:hi], back[:])

        for h in range(2):
            gate_pass(0, h)
        for which in range(2):
            for h in range(2):
                ha_passes(0, h, (which,))
        gate_pass(1, 0)
        for h in range(2):
            read_ha(0, h)
        for t in range(1, PACK):
            for h in range(int(t == 1), 2):
                gate_pass(t, h)
            for h in range(2):
                ha_passes(t, h)

        shared, rest = slice(0, SHARE), slice(SHARE, J)
        woven = {SHARE: keep.tile([P, J - SHARE, PACK], BF16, name="woven_rest", align_bytes=64)}

        def woven_cols(lo, hi):
            base = SHARE if lo >= SHARE else 0
            return woven[base][:, lo - base : hi - base, :]

        def round_lo(cols):
            nc.scalar.copy(out=woven_cols(cols.start, cols.stop)[:, :, 0:2], in_=y_lo[:, :, cols].rearrange("p t j -> p j t"))

        def round_hi(copy, lo, hi):
            copy(out=woven_cols(lo, hi)[:, :, 2:4], in_=y_hi[:, :, lo:hi].rearrange("p t j -> p j t"))

        new_kept(0, 0, J, "kept0_0")
        gather_r(0, 0, J)
        for t, h in ((1, 0), (1, 1), (2, 0)):
            read_ha(t, h)
        nc.gpsimd.tensor_tensor(y[0][:, shared], kept_cols(0, 0, SHARE), made[0, 0][:, shared], ALU.add)
        close_sum(0, SHARE, J, open_sum(0, SHARE, J, 3), 2)
        rest_of_set_1 = open_sum(1, SHARE, J, 4)
        quarters = ((0, HALF // 2), (HALF // 2, HALF))
        quarters_of_set_2 = [open_sum(2, lo, hi, 5 + i) for i, (lo, hi) in enumerate(quarters)]
        nc.sync.dma_start(out=y_rows[0], in_=y[0])

        for lo, hi in ((SHARE, J), (0, SHARE)):
            new_kept(1, lo, hi, f"kept1_{lo}")
            gather_r(1, lo, hi)
        close_sum(1, SHARE, J, rest_of_set_1, 4)
        round_lo(rest)
        woven[0] = tile([P, SHARE, PACK], BF16, "woven_shared", f"staged1_{SHARE}")
        for t, h in ((2, 1), (3, 0), (3, 1)):
            read_ha(t, h)
        for cols in (slice(0, SHARE // 2), slice(SHARE // 2, SHARE)):
            nc.gpsimd.tensor_tensor(y[1][:, cols], kept_cols(1, cols.start, cols.stop), made[1, 0][:, cols], ALU.add)
            round_lo(cols)
        nc.sync.dma_start(out=y_rows[1], in_=y[1])

        for lo, hi in ((0, HALF), (HALF, J)):
            new_kept(2, lo, hi, f"kept2_{lo}")
            gather_r(2, lo, hi)
        for i, (lo, hi) in enumerate(quarters):
            close_sum(2, lo, hi, quarters_of_set_2[i], 2 + i)
        blend(2, HALF, J)
        nc.sync.dma_start(out=y_rows[2], in_=y[2])

        y_w = keep.tile([P, J], U32, name="y_w", align_bytes=64)
        y_s = keep.tile([P, J], U8, name="y_s", align_bytes=64)
        words_out = out_1[0].rearrange("p j i -> p (j i)").bitcast(I32)
        last = PACK - 1
        pieces = [(lo, lo + PIECE) for lo in range(0, J, PIECE)]
        on_vector = len(pieces) - 2

        new_kept(last, 0, J, "carry1")
        gather_r(last, *pieces[0])
        for i, (lo, hi) in enumerate(pieces):
            if i + 1 < len(pieces):
                gather_r(last, *pieces[i + 1])
            blend(last, lo, hi)
            if i != on_vector:
                round_hi(nc.scalar.copy, lo, hi)
            if hi % HALF == 0:
                nc.sync.dma_start(out=y_rows[last][:, hi - HALF : hi], in_=y[last][:, hi - HALF : hi])
        round_hi(nc.vector.tensor_copy, *pieces[on_vector])
        for lo, hi in ((0, SHARE // 2), (SHARE // 2, SHARE), (SHARE, J)):
            nc.vector.quantize_mx(
                out=y_w[:, lo:hi].bitcast(FP8X4), scales=y_s[:, lo:hi], in_=woven_cols(lo, hi).rearrange("p j t -> p (j t)")
            )
            nc.sync.dma_start(out=words_out[:, lo:hi], in_=y_w[:, lo:hi].bitcast(I32))
        for r in range(QUADRANT // BLOCK):
            (nc.sync, nc.scalar)[r % 2].dma_start(
                out=out_2[0, r :: QUADRANT // BLOCK, :].bitcast(I32), in_=y_s[r:P:QUADRANT, :].bitcast(I32)
            )
